import numpy as np
import ml_dtypes


def mxq(x, axis, fmt="e4m3"):
    dtype, down = {"e4m3": (ml_dtypes.float8_e4m3fn, 7), "e5m2": (ml_dtypes.float8_e5m2, 14)}[fmt]
    v = np.moveaxis(np.asarray(x, np.float32).astype(ml_dtypes.bfloat16).astype(np.float64), axis, -1)
    blocks = v.reshape(v.shape[:-1] + (-1, 32))
    amax = np.abs(blocks).max(-1, keepdims=True)
    byte = np.maximum(np.where(amax > 0, np.frexp(amax)[1] - 1 + 127, 0) - down, 1)
    scale = np.exp2(byte - 127.0)
    codes = (blocks / scale).astype(np.float32).astype(dtype).astype(np.float64)
    return np.moveaxis((codes * scale).reshape(v.shape), -1, axis)


WIDE = False


def mx_kscale(k):
    if not WIDE:
        return np.ones(k)
    levels = np.array([10, -10, 5, -5, 0])
    if k % 512:
        return np.exp2(np.random.permutation(np.resize(levels, k // 32))).repeat(32)
    a = np.empty((k // 512, 16))
    for p in range(k // 512):
        a[p, :8] = np.random.permutation(np.resize(levels, 8))
        for g in range(8):
            far = levels[np.abs(levels - a[p, g]) >= 10]
            a[p, g + 8] = far[np.random.randint(len(far))]
    return np.exp2(a.ravel()).repeat(32)


def f64(x):
    return np.asarray(x).astype(np.float64)


def striped(idx):
    return np.tile(np.asarray(idx).reshape(-1, 16).T, (8, 1)).astype(np.uint16)


def unstriped(offs):
    return offs[:16].T.reshape(-1).astype(np.int64)


E2M1 = np.array([0.0, 0.5, 1.0, 1.5, 2.0, 3.0, 4.0, 6.0, -0.0, -0.5, -1.0, -1.5, -2.0, -3.0, -4.0, -6.0])


def pack_weight(w, fmt):
    k, n = w.shape
    w = f64(np.asarray(w, np.float32).astype(ml_dtypes.bfloat16)).reshape(k // 32, 32, n)
    amax = np.abs(w).max(1)
    if fmt == "e4m3":
        byte = np.frexp(amax)[1] - 1 + 127 - 7
    else:
        mant, ex = np.frexp(amax / 6.0)
        byte = np.where(mant > 0.5, ex, ex - 1) + 127
    byte = np.clip(np.where(amax > 0, byte, 1), 1, 254)
    scaled = (w * np.exp2(127.0 - byte)[:, None, :]).reshape(k, n).astype(np.float32)
    by_word = np.ascontiguousarray(scaled.reshape(k // 512, 128, 4, n).transpose(0, 1, 3, 2))
    if fmt == "e4m3":
        words = by_word.astype(ml_dtypes.float8_e4m3fn).view(np.uint8)
    else:
        c = by_word.astype(ml_dtypes.float4_e2m1fn).view(np.uint8) & 0xF
        words = (c[..., 0::2] | (c[..., 1::2] << 4)).reshape(k // 512, 128, 2 * n)
    return np.ascontiguousarray(words), np.ascontiguousarray(byte.astype(np.uint8).reshape(k // 512, 16, n))


def unpack_weight(words, scales, fmt):
    g, _, n = scales.shape
    words = np.ascontiguousarray(words).reshape(g, 128, n, -1)
    if fmt == "e4m3":
        vals = words.view(ml_dtypes.float8_e4m3fn).astype(np.float64)
    else:
        nib = np.empty((g, 128, n, 4), np.uint8)
        nib[..., 0::2] = words & 0xF
        nib[..., 1::2] = words >> 4
        vals = E2M1[nib]
    vals = vals * np.repeat(np.exp2(scales.astype(np.float64) - 127.0), 8, axis=1)[..., None]
    return vals.transpose(0, 1, 3, 2).reshape(g * 512, n)


B, N, T, D, NQ = 1, 512, 2048, 512, 512
SEG = 16


def setup_inputs():
    n = np.random.standard_normal
    idx = np.sort(np.random.permutation(T)[:B * N].reshape(B, N), axis=1).reshape(-1)
    s = mx_kscale(D)[:, None]
    kp = pack_weight(n((D, T)) / s, "e4m3")
    return {
        "qT": (n((B, D, NQ)) * s * (1.00 / np.sqrt(D))).astype(np.float32),
        "k_words": kp[0],
        "k_scales": kp[1],
        "bo": np.tile(np.random.uniform(0.0, 2.0, 2048), (128, 1)).astype(np.float32),
        "offs": striped(idx),
    }


def reference(qT, k_words, k_scales, bo, offs):
    idx = unstriped(offs)
    pick = lambda x, which: x[:, which].reshape(x.shape[0], B, -1).transpose(1, 0, 2)
    k = unpack_weight(k_words, k_scales, "e4m3")
    kg = pick(k, idx)
    qq = mxq(f64(qT), 1, "e4m3")
    a = kg.transpose(0, 2, 1) @ qq
    y = a.reshape(B, N, NQ // SEG, SEG).max(-1) + pick(f64(bo), idx)[:, :1, :].transpose(0, 2, 1)
    return y

@@ -1,0 +1,111 @@
+from contextlib import ExitStack
+
+import concourse.mybir as mybir
+from concourse.masks import make_identity
+
+F32 = mybir.dt.float32
+BF16 = mybir.dt.bfloat16
+I32 = mybir.dt.int32
+U32 = mybir.dt.uint32
+U16 = mybir.dt.uint16
+U8 = mybir.dt.uint8
+FP8X4 = mybir.dt.float8_e4m3fn_x4
+
+P = 128
+PACK = 4
+SLOTS, POOL, D, NQ, SEG = 512, 2048, 512, 512, 16
+RUNS = NQ // SEG
+TILES = SLOTS // P
+HALF = SLOTS // 2
+PREFIX = POOL - HALF
+LIVE = P - 1
+
+FLOPS = 2 * SLOTS * D * NQ
+BYTES = D * NQ * 4 + P * POOL * 4 + 16 * POOL + POOL * 4 + P * (SLOTS // 16) * 2 + SLOTS * RUNS * 4
+
+
+def tile_attend_tok_ucb_srt_kernel(tc, qT, k_words, k_scales, bo, offs, out):
+    nc = tc.nc
+    with ExitStack() as ctx:
+        sb = ctx.enter_context(tc.tile_pool(name="sb", bufs=1))
+        ps = ctx.enter_context(tc.psum_pool(name="ps", bufs=1))
+
+        offsets = sb.tile([P, SLOTS // 16], U16, name="offsets")
+        bonus_pool = sb.tile([P, POOL], F32, name="bonus_pool")
+        scale_pool = sb.tile([P, POOL], U8, name="scale_pool")
+        word_pool = sb.tile([P, POOL], U32, name="word_pool")
+        q_raw = sb.tile([P, PACK * NQ], F32, name="q_raw")
+        ident = sb.tile([P, P], F32, name="ident")
+
+        warm_in = sb.tile([P, 1], F32, name="warm_in")
+        warm_out = sb.tile([P, 1], BF16, name="warm_out")
+        nc.gpsimd.memset(warm_in[:], 0.0)
+        nc.scalar.copy(warm_out[:], warm_in[:])
+        nc.vector.memset(scale_pool[:].bitcast(I32), 0)
+        nc.vector.memset(bonus_pool[0:LIVE, :], 0.0)
+        make_identity(nc, ident[:])
+
+        q_rows = qT[0].rearrange("(p j) w -> p (j w)", j=PACK)
+        words = k_words[0].rearrange("p n t -> p (n t)").bitcast(I32)
+        scales = k_scales[0].bitcast(I32)
+        nc.sync.dma_start(offsets[:], offs)
+        nc.sync.dma_start(bonus_pool[LIVE:P, :], bo[LIVE:P, :])
+        nc.sync.dma_start(q_raw[:, 0 : 2 * NQ], q_rows[:, 0 : 2 * NQ])
+        for quad in range(4):
+            nc.sync.dma_start(scale_pool[32 * quad : 32 * quad + 4, :].bitcast(I32), scales[4 * quad : 4 * quad + 4, :])
+        nc.sync.dma_start(q_raw[:, 2 * NQ :], q_rows[:, 2 * NQ :])
+        nc.sync.dma_start(word_pool[:, 0:PREFIX].bitcast(I32), words[:, 0:PREFIX])
+        nc.sync.dma_start(word_pool[:, PREFIX:].bitcast(I32), words[:, PREFIX:])
+
+        bonus_row = sb.tile([P, SLOTS], F32, name="bonus_row")
+        nc.vector.tensor_copy(bonus_row[:], bonus_pool[:].indirect(offsets[:]))
+        k_scale = sb.tile([P, SLOTS], U8, name="k_scale", align_bytes=64)
+        nc.vector.tensor_copy(k_scale[:], scale_pool[:].indirect(offsets[:]))
+
+        bonus_col = ps.tile([P, TILES, P], F32, name="bonus_col")
+        for r in range(TILES):
+            nc.tensor.transpose(bonus_col[:, r, :], bonus_row[:, r * P : (r + 1) * P], ident[:])
+
+        q_codes = sb.tile([P, NQ], U32, name="q_codes", align_bytes=64)
+        q_scale = sb.tile([P, NQ], U8, name="q_scale", align_bytes=64)
+        q_view = q_raw[:].rearrange("p (t c i) -> p c t i", t=PACK, i=4)
+        width = NQ // 2
+        grouped = [sb.tile([P, width * PACK], BF16, name="grouped%d" % h, align_bytes=64) for h in range(2)]
+        for h in range(2):
+            dst = grouped[h][:].rearrange("p (c i t) -> p c t i", i=4, t=PACK)
+            src = q_view[:, h * width // 4 : (h + 1) * width // 4, :, :]
+            if h == 0:
+                nc.vector.tensor_copy(dst, src)
+            else:
+                nc.scalar.copy(dst, src)
+        for h in range(2):
+            cols = slice(h * width, (h + 1) * width)
+            nc.vector.quantize_mx(out=q_codes[:, cols].bitcast(FP8X4), scales=q_scale[:, cols], in_=grouped[h][:])
+
+        k_codes = [sb.tile([P, HALF], U32, name="k_codes%d" % h, align_bytes=64) for h in range(2)]
+        nc.vector.tensor_copy(k_codes[0][:], word_pool[:, 0:PREFIX].indirect(offsets[:, 0 : HALF // 16]))
+        nc.vector.tensor_copy(k_codes[1][:], word_pool[:].indirect(offsets[:, HALF // 16 :]))
+
+        best = sb.tile([P, TILES, RUNS], F32, name="best")
+        out_view = out[0].rearrange("(r p) j -> p r j", p=P)
+        for r in range(TILES):
+            scores = ps.tile([P, NQ], F32, name="scores%d" % r)
+            nc.tensor.matmul_mx(
+                out=scores[:],
+                lhsT=k_codes[r // 2][:, (r % 2) * P : (r % 2 + 1) * P].bitcast(FP8X4),
+                lhsT_scale=k_scale[:, r * P : (r + 1) * P],
+                rhs=q_codes[:].bitcast(FP8X4),
+                rhs_scale=q_scale[:],
+                start=True,
+                stop=True,
+            )
+            nc.vector.tensor_reduce(
+                best[:, r, :], scores[:].rearrange("p (j s) -> p j s", s=SEG), axis=mybir.AxisListType.X, op=mybir.AluOpType.max
+            )
+            if r % 2 == 1:
+                pair = slice(r - 1, r + 1)
+                result = sb.tile([P, 2, RUNS], F32, name="result%d" % r)
+                nc.vector.tensor_tensor(
+                    result[:], best[:, pair, :], bonus_col[:, pair, LIVE:P].to_broadcast([P, 2, RUNS]), mybir.AluOpType.add
+                )
+                nc.sync.dma_start(out_view[:, pair, :], result[:])

@@ -1,7 +1,6 @@
 from contextlib import ExitStack
 
 import concourse.mybir as mybir
-from concourse.masks import make_identity
 
 F32 = mybir.dt.float32
 BF16 = mybir.dt.bfloat16
@@ -19,6 +18,7 @@ TILES = SLOTS // P
 HALF = SLOTS // 2
 PREFIX = POOL - HALF
 LIVE = P - 1
+CHUNKS = ((0, 256), (256, 384), (384, 512))
 
 FLOPS = 2 * SLOTS * D * NQ
 BYTES = D * NQ * 4 + P * POOL * 4 + 16 * POOL + POOL * 4 + P * (SLOTS // 16) * 2 + SLOTS * RUNS * 4
@@ -28,84 +28,141 @@ def tile_attend_tok_ucb_srt_kernel(tc, qT, k_words, k_scales, bo, offs, out):
     nc = tc.nc
     with ExitStack() as ctx:
         sb = ctx.enter_context(tc.tile_pool(name="sb", bufs=1))
+        late = ctx.enter_context(tc.tile_pool(name="late", bufs=1))
         ps = ctx.enter_context(tc.psum_pool(name="ps", bufs=1))
 
         offsets = sb.tile([P, SLOTS // 16], U16, name="offsets")
         bonus_pool = sb.tile([P, POOL], F32, name="bonus_pool")
         scale_pool = sb.tile([P, POOL], U8, name="scale_pool")
-        word_pool = sb.tile([P, POOL], U32, name="word_pool")
-        q_raw = sb.tile([P, PACK * NQ], F32, name="q_raw")
         ident = sb.tile([P, P], F32, name="ident")
 
-        warm_in = sb.tile([P, 1], F32, name="warm_in")
-        warm_out = sb.tile([P, 1], BF16, name="warm_out")
-        nc.gpsimd.memset(warm_in[:], 0.0)
-        nc.scalar.copy(warm_out[:], warm_in[:])
-        nc.vector.memset(scale_pool[:].bitcast(I32), 0)
-        nc.vector.memset(bonus_pool[0:LIVE, :], 0.0)
-        make_identity(nc, ident[:])
+        zeros = late.tile([P, P], F32, name="zeros", offset=POOL * 4 - 256)
+        nc.vector.memset(scale_pool[:, 0 : POOL // 2].bitcast(I32), 0)
+        nc.gpsimd.memset(scale_pool[:, POOL // 2 :].bitcast(I32), 0)
+        nc.gpsimd.memset(zeros[:], 0.0)
+        nc.gpsimd.affine_select(
+            out=ident[:],
+            in_=zeros[:],
+            compare_op=mybir.AluOpType.not_equal,
+            fill=1.0,
+            base=0,
+            pattern=[[-1, P]],
+            channel_multiplier=1,
+        )
+        for lo in range(0, POOL, 512):
+            nc.vector.memset(bonus_pool[0:LIVE, lo : lo + 512], 0.0)
+        word_pool = late.tile([P, POOL], U32, name="word_pool", offset=0)
+        q_early = sb.tile([P, PACK * 256], F32, name="q_early")
+        q_late = late.tile([P, PACK * 256], F32, name="q_late", offset=POOL * 4)
+        q_raw = [
+            q_early[:].rearrange("p (t w) -> p t w", t=PACK),
+            q_late[:, 0:512].rearrange("p (t w) -> p t w", t=PACK),
+            q_late[:, 512:].rearrange("p (t w) -> p t w", t=PACK),
+        ]
 
-        q_rows = qT[0].rearrange("(p j) w -> p (j w)", j=PACK)
+        q_rows = qT[0].rearrange("(p j) w -> p j w", j=PACK)
         words = k_words[0].rearrange("p n t -> p (n t)").bitcast(I32)
         scales = k_scales[0].bitcast(I32)
+
+        def load_q(c):
+            lo, hi = CHUNKS[c]
+            nc.sync.dma_start(q_raw[c], q_rows[:, :, lo:hi])
+
+        def load_scales():
+            for quad in range(4):
+                queue = nc.sync if quad % 2 == 0 else nc.scalar
+                queue.dma_start(scale_pool[32 * quad : 32 * quad + 4, :].bitcast(I32), scales[4 * quad : 4 * quad + 4, :])
+
+        def load_words(lo, hi):
+            nc.sync.dma_start(word_pool[:, lo:hi].bitcast(I32), words[:, lo:hi])
+
         nc.sync.dma_start(offsets[:], offs)
-        nc.sync.dma_start(bonus_pool[LIVE:P, :], bo[LIVE:P, :])
-        nc.sync.dma_start(q_raw[:, 0 : 2 * NQ], q_rows[:, 0 : 2 * NQ])
-        for quad in range(4):
-            nc.sync.dma_start(scale_pool[32 * quad : 32 * quad + 4, :].bitcast(I32), scales[4 * quad : 4 * quad + 4, :])
-        nc.sync.dma_start(q_raw[:, 2 * NQ :], q_rows[:, 2 * NQ :])
-        nc.sync.dma_start(word_pool[:, 0:PREFIX].bitcast(I32), words[:, 0:PREFIX])
-        nc.sync.dma_start(word_pool[:, PREFIX:].bitcast(I32), words[:, PREFIX:])
+        nc.scalar.dma_start(bonus_pool[LIVE:P, :], bo[LIVE:P, :])
+        load_q(0)
+        load_scales()
+        load_words(0, PREFIX)
+        load_words(PREFIX, POOL)
+        load_q(1)
+        load_q(2)
 
         bonus_row = sb.tile([P, SLOTS], F32, name="bonus_row")
-        nc.vector.tensor_copy(bonus_row[:], bonus_pool[:].indirect(offsets[:]))
         k_scale = sb.tile([P, SLOTS], U8, name="k_scale", align_bytes=64)
-        nc.vector.tensor_copy(k_scale[:], scale_pool[:].indirect(offsets[:]))
-
-        bonus_col = ps.tile([P, TILES, P], F32, name="bonus_col")
-        for r in range(TILES):
-            nc.tensor.transpose(bonus_col[:, r, :], bonus_row[:, r * P : (r + 1) * P], ident[:])
-
-        q_codes = sb.tile([P, NQ], U32, name="q_codes", align_bytes=64)
-        q_scale = sb.tile([P, NQ], U8, name="q_scale", align_bytes=64)
-        q_view = q_raw[:].rearrange("p (t c i) -> p c t i", t=PACK, i=4)
-        width = NQ // 2
-        grouped = [sb.tile([P, width * PACK], BF16, name="grouped%d" % h, align_bytes=64) for h in range(2)]
-        for h in range(2):
-            dst = grouped[h][:].rearrange("p (c i t) -> p c t i", i=4, t=PACK)
-            src = q_view[:, h * width // 4 : (h + 1) * width // 4, :, :]
-            if h == 0:
-                nc.vector.tensor_copy(dst, src)
-            else:
-                nc.scalar.copy(dst, src)
-        for h in range(2):
-            cols = slice(h * width, (h + 1) * width)
-            nc.vector.quantize_mx(out=q_codes[:, cols].bitcast(FP8X4), scales=q_scale[:, cols], in_=grouped[h][:])
-
         k_codes = [sb.tile([P, HALF], U32, name="k_codes%d" % h, align_bytes=64) for h in range(2)]
-        nc.vector.tensor_copy(k_codes[0][:], word_pool[:, 0:PREFIX].indirect(offsets[:, 0 : HALF // 16]))
-        nc.vector.tensor_copy(k_codes[1][:], word_pool[:].indirect(offsets[:, HALF // 16 :]))
-
-        best = sb.tile([P, TILES, RUNS], F32, name="best")
+        bonus_col = ps.tile([P, TILES, P], F32, name="bonus_col")
+        room = [sb.tile([P, 128 + (hi - lo) * PACK], BF16, name="room%d" % lo, align_bytes=64) for lo, hi in CHUNKS]
+        grouped = [t[:, 128:] for t in room]
+        q_codes = [sb.tile([P, hi - lo], U32, name="q_codes%d" % lo, align_bytes=64) for lo, hi in CHUNKS]
+        q_scale = [sb.tile([P, hi - lo], U8, name="q_scale%d" % lo, align_bytes=64) for lo, hi in CHUNKS]
+        best = [
+            room[2][:, 64:192].bitcast(F32).rearrange("p (j i) -> p i j", i=2),
+            room[1][:, 128:256].bitcast(F32).rearrange("p (j i) -> p i j", i=2),
+        ]
         out_view = out[0].rearrange("(r p) j -> p r j", p=P)
-        for r in range(TILES):
-            scores = ps.tile([P, NQ], F32, name="scores%d" % r)
-            nc.tensor.matmul_mx(
-                out=scores[:],
-                lhsT=k_codes[r // 2][:, (r % 2) * P : (r % 2 + 1) * P].bitcast(FP8X4),
-                lhsT_scale=k_scale[:, r * P : (r + 1) * P],
-                rhs=q_codes[:].bitcast(FP8X4),
-                rhs_scale=q_scale[:],
-                start=True,
-                stop=True,
+
+        def gather_bonus():
+            nc.vector.tensor_copy(bonus_row[:], bonus_pool[:].indirect(offsets[:]))
+            for r in range(TILES):
+                nc.tensor.transpose(bonus_col[:, r, :], bonus_row[:, r * P : (r + 1) * P], ident[:])
+
+        def gather_scales():
+            nc.vector.tensor_copy(k_scale[:], scale_pool[:].indirect(offsets[:]))
+
+        def gather_words():
+            nc.vector.tensor_copy(k_codes[0][:], word_pool[:, 0:PREFIX].indirect(offsets[:, 0 : HALF // 16]))
+            nc.vector.tensor_copy(k_codes[1][:], word_pool[:].indirect(offsets[:, HALF // 16 :]))
+
+        def interleave(c):
+            nc.scalar.copy(
+                grouped[c].rearrange("p (c i t) -> p c t i", i=4, t=PACK),
+                q_raw[c].rearrange("p t (c i) -> p c t i", i=4),
             )
-            nc.vector.tensor_reduce(
-                best[:, r, :], scores[:].rearrange("p (j s) -> p j s", s=SEG), axis=mybir.AxisListType.X, op=mybir.AluOpType.max
-            )
-            if r % 2 == 1:
-                pair = slice(r - 1, r + 1)
-                result = sb.tile([P, 2, RUNS], F32, name="result%d" % r)
-                nc.vector.tensor_tensor(
-                    result[:], best[:, pair, :], bonus_col[:, pair, LIVE:P].to_broadcast([P, 2, RUNS]), mybir.AluOpType.add
+
+        def quantise(c):
+            nc.vector.quantize_mx(out=q_codes[c][:].bitcast(FP8X4), scales=q_scale[c][:], in_=grouped[c])
+
+        def score(c, h):
+            lo, hi = CHUNKS[c]
+            bank = ps.tile([P, 2, hi - lo], F32, name="scores%d_%d" % (c, h))
+            for i in range(2):
+                r = 2 * h + i
+                nc.tensor.matmul_mx(
+                    out=bank[:, i, :],
+                    lhsT=k_codes[h][:, i * P : (i + 1) * P].bitcast(FP8X4),
+                    lhsT_scale=k_scale[:, r * P : (r + 1) * P],
+                    rhs=q_codes[c][:].bitcast(FP8X4),
+                    rhs_scale=q_scale[c][:],
+                    start=True,
+                    stop=True,
                 )
-                nc.sync.dma_start(out_view[:, pair, :], result[:])
+            nc.vector.tensor_reduce(
+                best[h][:, :, lo // SEG : hi // SEG],
+                bank[:].rearrange("p i (j s) -> p i j s", s=SEG),
+                axis=mybir.AxisListType.X,
+                op=mybir.AluOpType.max,
+            )
+
+        def finish(h):
+            pair = slice(2 * h, 2 * h + 2)
+            result = sb.tile([P, 2, RUNS], F32, name="result%d" % h)
+            nc.vector.tensor_tensor(
+                result[:], best[h], bonus_col[:, pair, LIVE:P].to_broadcast([P, 2, RUNS]), mybir.AluOpType.add
+            )
+            nc.sync.dma_start(out_view[:, pair, :], result[:])
+
+        gather_bonus()
+        gather_scales()
+        interleave(0)
+        interleave(1)
+        interleave(2)
+        quantise(0)
+        gather_words()
+        quantise(1)
+        quantise(2)
+        score(0, 0)
+        score(0, 1)
+        score(1, 0)
+        score(1, 1)
+        score(2, 0)
+        finish(0)
+        score(2, 1)
+        finish(1)

@@ -16,12 +16,17 @@ SLOTS, POOL, D, NQ, SEG = 512, 2048, 512, 512, 16
 RUNS = NQ // SEG
 TILES = SLOTS // P
 HALF = SLOTS // 2
+LIST_ROWS = 16
+QUADRANTS = 4
 PREFIX = POOL - HALF
 LIVE = P - 1
+CLEAR = 512
 CHUNKS = ((0, 256), (256, 384), (384, 512))
+EARLY = CHUNKS[0][1]
+LEAD = 128
 
 FLOPS = 2 * SLOTS * D * NQ
-BYTES = D * NQ * 4 + P * POOL * 4 + 16 * POOL + POOL * 4 + P * (SLOTS // 16) * 2 + SLOTS * RUNS * 4
+BYTES = D * NQ * 4 + P * POOL * 4 + (D // 32) * POOL + POOL * 4 + P * (SLOTS // LIST_ROWS) * 2 + SLOTS * RUNS * 4
 
 
 def tile_attend_tok_ucb_srt_kernel(tc, qT, k_words, k_scales, bo, offs, out):
@@ -31,12 +36,12 @@ def tile_attend_tok_ucb_srt_kernel(tc, qT, k_words, k_scales, bo, offs, out):
         late = ctx.enter_context(tc.tile_pool(name="late", bufs=1))
         ps = ctx.enter_context(tc.psum_pool(name="ps", bufs=1))
 
-        offsets = sb.tile([P, SLOTS // 16], U16, name="offsets")
+        offsets = sb.tile([P, SLOTS // LIST_ROWS], U16, name="offsets")
         bonus_pool = sb.tile([P, POOL], F32, name="bonus_pool")
         scale_pool = sb.tile([P, POOL], U8, name="scale_pool")
         ident = sb.tile([P, P], F32, name="ident")
 
-        zeros = late.tile([P, P], F32, name="zeros", offset=POOL * 4 - 256)
+        zeros = late.tile([P, P], F32, name="zeros", offset=POOL * 4 - P * 2)
         nc.vector.memset(scale_pool[:, 0 : POOL // 2].bitcast(I32), 0)
         nc.gpsimd.memset(scale_pool[:, POOL // 2 :].bitcast(I32), 0)
         nc.gpsimd.memset(zeros[:], 0.0)
@@ -49,18 +54,17 @@ def tile_attend_tok_ucb_srt_kernel(tc, qT, k_words, k_scales, bo, offs, out):
             pattern=[[-1, P]],
             channel_multiplier=1,
         )
-        for lo in range(0, POOL, 512):
-            nc.vector.memset(bonus_pool[0:LIVE, lo : lo + 512], 0.0)
+        for lo in range(0, POOL, CLEAR):
+            nc.vector.memset(bonus_pool[0:LIVE, lo : lo + CLEAR], 0.0)
         word_pool = late.tile([P, POOL], U32, name="word_pool", offset=0)
-        q_early = sb.tile([P, PACK * 256], F32, name="q_early")
-        q_late = late.tile([P, PACK * 256], F32, name="q_late", offset=POOL * 4)
-        q_raw = [
-            q_early[:].rearrange("p (t w) -> p t w", t=PACK),
-            q_late[:, 0:512].rearrange("p (t w) -> p t w", t=PACK),
-            q_late[:, 512:].rearrange("p (t w) -> p t w", t=PACK),
+        q_early = sb.tile([P, PACK * EARLY], F32, name="q_early")
+        q_late = late.tile([P, PACK * (NQ - EARLY)], F32, name="q_late", offset=POOL * 4)
+        q_raw = [q_early[:].rearrange("p (t w) -> p t w", t=PACK)] + [
+            q_late[:, PACK * (lo - EARLY) : PACK * (hi - EARLY)].rearrange("p (t w) -> p t w", t=PACK)
+            for lo, hi in CHUNKS[1:]
         ]
 
-        q_rows = qT[0].rearrange("(p j) w -> p j w", j=PACK)
+        q_rows = qT[0].rearrange("(p t) w -> p t w", t=PACK)
         words = k_words[0].rearrange("p n t -> p (n t)").bitcast(I32)
         scales = k_scales[0].bitcast(I32)
 
@@ -68,20 +72,13 @@ def tile_attend_tok_ucb_srt_kernel(tc, qT, k_words, k_scales, bo, offs, out):
             lo, hi = CHUNKS[c]
             nc.sync.dma_start(q_raw[c], q_rows[:, :, lo:hi])
 
-        def load_scales():
-            for quad in range(4):
-                queue = nc.sync if quad % 2 == 0 else nc.scalar
-                queue.dma_start(scale_pool[32 * quad : 32 * quad + 4, :].bitcast(I32), scales[4 * quad : 4 * quad + 4, :])
-
-        def load_words(lo, hi):
-            nc.sync.dma_start(word_pool[:, lo:hi].bitcast(I32), words[:, lo:hi])
-
         nc.sync.dma_start(offsets[:], offs)
-        nc.scalar.dma_start(bonus_pool[LIVE:P, :], bo[LIVE:P, :])
+        nc.sync.dma_start(bonus_pool[LIVE:P, :], bo[LIVE:P, :])
         load_q(0)
-        load_scales()
-        load_words(0, PREFIX)
-        load_words(PREFIX, POOL)
+        for quad in range(QUADRANTS):
+            nc.sync.dma_start(scale_pool[32 * quad : 32 * quad + 4, :].bitcast(I32), scales[4 * quad : 4 * quad + 4, :])
+        for lo, hi in ((0, PREFIX), (PREFIX, POOL)):
+            nc.sync.dma_start(word_pool[:, lo:hi].bitcast(I32), words[:, lo:hi])
         load_q(1)
         load_q(2)
 
@@ -89,36 +86,15 @@ def tile_attend_tok_ucb_srt_kernel(tc, qT, k_words, k_scales, bo, offs, out):
         k_scale = sb.tile([P, SLOTS], U8, name="k_scale", align_bytes=64)
         k_codes = [sb.tile([P, HALF], U32, name="k_codes%d" % h, align_bytes=64) for h in range(2)]
         bonus_col = ps.tile([P, TILES, P], F32, name="bonus_col")
-        room = [sb.tile([P, 128 + (hi - lo) * PACK], BF16, name="room%d" % lo, align_bytes=64) for lo, hi in CHUNKS]
-        grouped = [t[:, 128:] for t in room]
+        room = [sb.tile([P, LEAD + (hi - lo) * PACK], BF16, name="room%d" % lo, align_bytes=64) for lo, hi in CHUNKS]
+        grouped = [t[:, LEAD:] for t in room]
         q_codes = [sb.tile([P, hi - lo], U32, name="q_codes%d" % lo, align_bytes=64) for lo, hi in CHUNKS]
         q_scale = [sb.tile([P, hi - lo], U8, name="q_scale%d" % lo, align_bytes=64) for lo, hi in CHUNKS]
         best = [
-            room[2][:, 64:192].bitcast(F32).rearrange("p (j i) -> p i j", i=2),
-            room[1][:, 128:256].bitcast(F32).rearrange("p (j i) -> p i j", i=2),
+            room[2][:, LEAD - 2 * RUNS : LEAD + 2 * RUNS].bitcast(F32).rearrange("p (j i) -> p i j", i=2),
+            room[1][:, LEAD : LEAD + 4 * RUNS].bitcast(F32).rearrange("p (j i) -> p i j", i=2),
         ]
         out_view = out[0].rearrange("(r p) j -> p r j", p=P)
-
-        def gather_bonus():
-            nc.vector.tensor_copy(bonus_row[:], bonus_pool[:].indirect(offsets[:]))
-            for r in range(TILES):
-                nc.tensor.transpose(bonus_col[:, r, :], bonus_row[:, r * P : (r + 1) * P], ident[:])
-
-        def gather_scales():
-            nc.vector.tensor_copy(k_scale[:], scale_pool[:].indirect(offsets[:]))
-
-        def gather_words():
-            nc.vector.tensor_copy(k_codes[0][:], word_pool[:, 0:PREFIX].indirect(offsets[:, 0 : HALF // 16]))
-            nc.vector.tensor_copy(k_codes[1][:], word_pool[:].indirect(offsets[:, HALF // 16 :]))
-
-        def interleave(c):
-            nc.scalar.copy(
-                grouped[c].rearrange("p (c i t) -> p c t i", i=4, t=PACK),
-                q_raw[c].rearrange("p t (c i) -> p c t i", i=4),
-            )
-
-        def quantise(c):
-            nc.vector.quantize_mx(out=q_codes[c][:].bitcast(FP8X4), scales=q_scale[c][:], in_=grouped[c])
 
         def score(c, h):
             lo, hi = CHUNKS[c]
@@ -149,20 +125,30 @@ def tile_attend_tok_ucb_srt_kernel(tc, qT, k_words, k_scales, bo, offs, out):
             )
             nc.sync.dma_start(out_view[:, pair, :], result[:])
 
-        gather_bonus()
-        gather_scales()
-        interleave(0)
-        interleave(1)
-        interleave(2)
+        nc.vector.tensor_copy(bonus_row[:], bonus_pool[:].indirect(offsets[:]))
+        for r in range(TILES):
+            nc.tensor.transpose(bonus_col[:, r, :], bonus_row[:, r * P : (r + 1) * P], ident[:])
+        nc.vector.tensor_copy(k_scale[:], scale_pool[:].indirect(offsets[:]))
+
+        for c in range(len(CHUNKS)):
+            nc.scalar.copy(
+                grouped[c].rearrange("p (w i t) -> p w t i", i=4, t=PACK),
+                q_raw[c].rearrange("p t (w i) -> p w t i", i=4),
+            )
+
+        def quantise(c):
+            nc.vector.quantize_mx(out=q_codes[c][:].bitcast(FP8X4), scales=q_scale[c][:], in_=grouped[c])
+
         quantise(0)
-        gather_words()
+        nc.vector.tensor_copy(k_codes[0][:], word_pool[:, 0:PREFIX].indirect(offsets[:, 0 : HALF // LIST_ROWS]))
+        nc.vector.tensor_copy(k_codes[1][:], word_pool[:].indirect(offsets[:, HALF // LIST_ROWS :]))
         quantise(1)
         quantise(2)
-        score(0, 0)
-        score(0, 1)
-        score(1, 0)
-        score(1, 1)
-        score(2, 0)
-        finish(0)
-        score(2, 1)
-        finish(1)
+
+        last = len(CHUNKS) - 1
+        for c in range(last):
+            for h in range(2):
+                score(c, h)
+        for h in range(2):
+            score(last, h)
+            finish(h)

@@ -75,8 +75,8 @@ def tile_attend_tok_ucb_srt_kernel(tc, qT, k_words, k_scales, bo, offs, out):
         nc.sync.dma_start(offsets[:], offs)
         nc.sync.dma_start(bonus_pool[LIVE:P, :], bo[LIVE:P, :])
         load_q(0)
-        for quad in range(QUADRANTS):
-            nc.sync.dma_start(scale_pool[32 * quad : 32 * quad + 4, :].bitcast(I32), scales[4 * quad : 4 * quad + 4, :])
+        for r in range(4):
+            nc.sync.dma_start(scale_pool[r:P:32, :].bitcast(I32), scales[r : 4 * QUADRANTS : 4, :])
         for lo, hi in ((0, PREFIX), (PREFIX, POOL)):
             nc.sync.dma_start(word_pool[:, lo:hi].bitcast(I32), words[:, lo:hi])
         load_q(1)

@@ -20,7 +20,7 @@ LIST_ROWS = 16
 QUADRANTS = 4
 PREFIX = POOL - HALF
 LIVE = P - 1
-CLEAR = 512
+SCALE_ROW0 = P - D // 32
 CHUNKS = ((0, 256), (256, 384), (384, 512))
 EARLY = CHUNKS[0][1]
 LEAD = 128
@@ -38,12 +38,14 @@ def tile_attend_tok_ucb_srt_kernel(tc, qT, k_words, k_scales, bo, offs, out):
 
         offsets = sb.tile([P, SLOTS // LIST_ROWS], U16, name="offsets")
         bonus_pool = sb.tile([P, POOL], F32, name="bonus_pool")
-        scale_pool = sb.tile([P, POOL], U8, name="scale_pool")
+        scale_pool = late.tile([P, POOL], U8, name="scale_pool", offset=0)
+        k_scale = sb.tile([P, SLOTS], U8, name="k_scale", align_bytes=64)
         ident = sb.tile([P, P], F32, name="ident")
 
-        zeros = late.tile([P, P], F32, name="zeros", offset=POOL * 4 - P * 2)
-        nc.vector.memset(scale_pool[:, 0 : POOL // 2].bitcast(I32), 0)
-        nc.gpsimd.memset(scale_pool[:, POOL // 2 :].bitcast(I32), 0)
+        zeros = sb.tile([P, P], F32, name="zeros")
+        nc.vector.memset(scale_pool[0:SCALE_ROW0, :].bitcast(I32), 0)
+        nc.vector.memset(bonus_pool[0:LIVE, :], 0.0)
+        nc.gpsimd.memset(k_scale[:].bitcast(I32), 0)
         nc.gpsimd.memset(zeros[:], 0.0)
         nc.gpsimd.affine_select(
             out=ident[:],
@@ -54,11 +56,9 @@ def tile_attend_tok_ucb_srt_kernel(tc, qT, k_words, k_scales, bo, offs, out):
             pattern=[[-1, P]],
             channel_multiplier=1,
         )
-        for lo in range(0, POOL, CLEAR):
-            nc.vector.memset(bonus_pool[0:LIVE, lo : lo + CLEAR], 0.0)
-        word_pool = late.tile([P, POOL], U32, name="word_pool", offset=0)
+        word_pool = sb.tile([P, POOL], U32, name="word_pool")
         q_early = sb.tile([P, PACK * EARLY], F32, name="q_early")
-        q_late = late.tile([P, PACK * (NQ - EARLY)], F32, name="q_late", offset=POOL * 4)
+        q_late = late.tile([P, PACK * (NQ - EARLY)], F32, name="q_late", offset=0)
         q_raw = [q_early[:].rearrange("p (t w) -> p t w", t=PACK)] + [
             q_late[:, PACK * (lo - EARLY) : PACK * (hi - EARLY)].rearrange("p (t w) -> p t w", t=PACK)
             for lo, hi in CHUNKS[1:]
@@ -73,17 +73,14 @@ def tile_attend_tok_ucb_srt_kernel(tc, qT, k_words, k_scales, bo, offs, out):
             nc.sync.dma_start(q_raw[c], q_rows[:, :, lo:hi])
 
         nc.sync.dma_start(offsets[:], offs)
+        nc.sync.dma_start(scale_pool[SCALE_ROW0:P, :].bitcast(I32), scales)
         nc.sync.dma_start(bonus_pool[LIVE:P, :], bo[LIVE:P, :])
         load_q(0)
-        for r in range(4):
-            nc.sync.dma_start(scale_pool[r:P:32, :].bitcast(I32), scales[r : 4 * QUADRANTS : 4, :])
         for lo, hi in ((0, PREFIX), (PREFIX, POOL)):
             nc.sync.dma_start(word_pool[:, lo:hi].bitcast(I32), words[:, lo:hi])
-        load_q(1)
-        load_q(2)
 
         bonus_row = sb.tile([P, SLOTS], F32, name="bonus_row")
-        k_scale = sb.tile([P, SLOTS], U8, name="k_scale", align_bytes=64)
+        picked = sb.tile([P, SLOTS], U8, name="picked")
         k_codes = [sb.tile([P, HALF], U32, name="k_codes%d" % h, align_bytes=64) for h in range(2)]
         bonus_col = ps.tile([P, TILES, P], F32, name="bonus_col")
         room = [sb.tile([P, LEAD + (hi - lo) * PACK], BF16, name="room%d" % lo, align_bytes=64) for lo, hi in CHUNKS]
@@ -125,10 +122,16 @@ def tile_attend_tok_ucb_srt_kernel(tc, qT, k_words, k_scales, bo, offs, out):
             )
             nc.sync.dma_start(out_view[:, pair, :], result[:])
 
+        nc.vector.tensor_copy(picked[:], scale_pool[:].indirect(offsets[:]))
+        for quad in range(QUADRANTS):
+            rows = SCALE_ROW0 + 4 * quad
+            nc.sync.dma_start(k_scale[32 * quad : 32 * quad + 4, :].bitcast(I32), picked[rows : rows + 4, :].bitcast(I32))
+        load_q(1)
+        load_q(2)
+
         nc.vector.tensor_copy(bonus_row[:], bonus_pool[:].indirect(offsets[:]))
         for r in range(TILES):
             nc.tensor.transpose(bonus_col[:, r, :], bonus_row[:, r * P : (r + 1) * P], ident[:])
-        nc.vector.tensor_copy(k_scale[:], scale_pool[:].indirect(offsets[:]))
 
         for c in range(len(CHUNKS)):
             nc.scalar.copy(
@@ -145,10 +148,8 @@ def tile_attend_tok_ucb_srt_kernel(tc, qT, k_words, k_scales, bo, offs, out):
         quantise(1)
         quantise(2)
 
-        last = len(CHUNKS) - 1
-        for c in range(last):
+        for c in range(len(CHUNKS)):
             for h in range(2):
                 score(c, h)
         for h in range(2):
-            score(last, h)
             finish(h)

@@ -23,7 +23,9 @@ LIVE = P - 1
 SCALE_ROW0 = P - D // 32
 CHUNKS = ((0, 256), (256, 384), (384, 512))
 EARLY = CHUNKS[0][1]
-LEAD = 128
+UNIT = 128
+UNITS = NQ // UNIT
+UNIT_RUNS = UNIT // SEG
 
 FLOPS = 2 * SLOTS * D * NQ
 BYTES = D * NQ * 4 + P * POOL * 4 + (D // 32) * POOL + POOL * 4 + P * (SLOTS // LIST_ROWS) * 2 + SLOTS * RUNS * 4
@@ -56,13 +58,10 @@ def tile_attend_tok_ucb_srt_kernel(tc, qT, k_words, k_scales, bo, offs, out):
             pattern=[[-1, P]],
             channel_multiplier=1,
         )
-        word_pool = sb.tile([P, POOL], U32, name="word_pool")
-        q_early = sb.tile([P, PACK * EARLY], F32, name="q_early")
-        q_late = late.tile([P, PACK * (NQ - EARLY)], F32, name="q_late", offset=0)
-        q_raw = [q_early[:].rearrange("p (t w) -> p t w", t=PACK)] + [
-            q_late[:, PACK * (lo - EARLY) : PACK * (hi - EARLY)].rearrange("p (t w) -> p t w", t=PACK)
-            for lo, hi in CHUNKS[1:]
-        ]
+        word_pool = late.tile([P, POOL], U32, name="word_pool", offset=POOL)
+        q_tiles = [sb.tile([P, PACK * (hi - lo)], F32, name="q_raw%d" % lo) for lo, hi in CHUNKS[:-1]]
+        q_tiles.append(late.tile([P, PACK * (NQ - CHUNKS[-1][0])], F32, name="q_last", offset=0))
+        q_raw = [t[:].rearrange("p (t w) -> p t w", t=PACK) for t in q_tiles]
 
         q_rows = qT[0].rearrange("(p t) w -> p t w", t=PACK)
         words = k_words[0].rearrange("p n t -> p (n t)").bitcast(I32)
@@ -78,28 +77,35 @@ def tile_attend_tok_ucb_srt_kernel(tc, qT, k_words, k_scales, bo, offs, out):
         load_q(0)
         for lo, hi in ((0, PREFIX), (PREFIX, POOL)):
             nc.sync.dma_start(word_pool[:, lo:hi].bitcast(I32), words[:, lo:hi])
+        load_q(1)
 
         bonus_row = sb.tile([P, SLOTS], F32, name="bonus_row")
         picked = sb.tile([P, SLOTS], U8, name="picked")
         k_codes = [sb.tile([P, HALF], U32, name="k_codes%d" % h, align_bytes=64) for h in range(2)]
         bonus_col = ps.tile([P, TILES, P], F32, name="bonus_col")
-        room = [sb.tile([P, LEAD + (hi - lo) * PACK], BF16, name="room%d" % lo, align_bytes=64) for lo, hi in CHUNKS]
-        grouped = [t[:, LEAD:] for t in room]
-        q_codes = [sb.tile([P, hi - lo], U32, name="q_codes%d" % lo, align_bytes=64) for lo, hi in CHUNKS]
-        q_scale = [sb.tile([P, hi - lo], U8, name="q_scale%d" % lo, align_bytes=64) for lo, hi in CHUNKS]
-        best = [
-            room[2][:, LEAD - 2 * RUNS : LEAD + 2 * RUNS].bitcast(F32).rearrange("p (j i) -> p i j", i=2),
-            room[1][:, LEAD : LEAD + 4 * RUNS].bitcast(F32).rearrange("p (j i) -> p i j", i=2),
+        room = sb.tile([P, (NQ + UNIT) * PACK], BF16, name="room", align_bytes=64)
+        grouped = [room[:, lo * PACK : hi * PACK] for lo, hi in CHUNKS]
+        q_codes = [sb.tile([P, EARLY], U32, name="q_codes0", align_bytes=64)] + [
+            late.tile([P, hi - lo], U32, name="q_codes%d" % lo, align_bytes=64, offset=POOL + lo * 4)
+            for lo, hi in CHUNKS[1:]
         ]
+        q_scale = [sb.tile([P, hi - lo], U8, name="q_scale%d" % lo, align_bytes=64) for lo, hi in CHUNKS]
+        span = TILES * UNIT_RUNS
+        best = (
+            room[:, UNIT * PACK - span : (NQ + UNIT) * PACK - span]
+            .bitcast(F32)
+            .rearrange("p (u x) -> p u x", u=UNITS)[:, :, 0:span]
+            .rearrange("p u (r j) -> p r u j", r=TILES)
+        )
         out_view = out[0].rearrange("(r p) j -> p r j", p=P)
 
-        def score(c, h):
+        def score(c, first, last):
             lo, hi = CHUNKS[c]
-            bank = ps.tile([P, 2, hi - lo], F32, name="scores%d_%d" % (c, h))
-            for i in range(2):
-                r = 2 * h + i
+            bank = ps.tile([P, last - first, hi - lo], F32, name="scores%d_%d" % (c, first))
+            for r in range(first, last):
+                h, i = divmod(r, 2)
                 nc.tensor.matmul_mx(
-                    out=bank[:, i, :],
+                    out=bank[:, r - first, :],
                     lhsT=k_codes[h][:, i * P : (i + 1) * P].bitcast(FP8X4),
                     lhsT_scale=k_scale[:, r * P : (r + 1) * P],
                     rhs=q_codes[c][:].bitcast(FP8X4),
@@ -108,8 +114,8 @@ def tile_attend_tok_ucb_srt_kernel(tc, qT, k_words, k_scales, bo, offs, out):
                     stop=True,
                 )
             nc.vector.tensor_reduce(
-                best[h][:, :, lo // SEG : hi // SEG],
-                bank[:].rearrange("p i (j s) -> p i j s", s=SEG),
+                best[:, first:last, lo // UNIT : hi // UNIT, :],
+                bank[:].rearrange("p i (u j s) -> p i u j s", j=UNIT_RUNS, s=SEG),
                 axis=mybir.AxisListType.X,
                 op=mybir.AluOpType.max,
             )
@@ -118,7 +124,10 @@ def tile_attend_tok_ucb_srt_kernel(tc, qT, k_words, k_scales, bo, offs, out):
             pair = slice(2 * h, 2 * h + 2)
             result = sb.tile([P, 2, RUNS], F32, name="result%d" % h)
             nc.vector.tensor_tensor(
-                result[:], best[h], bonus_col[:, pair, LIVE:P].to_broadcast([P, 2, RUNS]), mybir.AluOpType.add
+                result[:].rearrange("p i (u j) -> p i u j", u=UNITS),
+                best[:, pair, :, :],
+                bonus_col[:, pair, LIVE:P].unsqueeze(3).to_broadcast([P, 2, UNITS, UNIT_RUNS]),
+                mybir.AluOpType.add,
             )
             nc.sync.dma_start(out_view[:, pair, :], result[:])
 
@@ -126,7 +135,6 @@ def tile_attend_tok_ucb_srt_kernel(tc, qT, k_words, k_scales, bo, offs, out):
         for quad in range(QUADRANTS):
             rows = SCALE_ROW0 + 4 * quad
             nc.sync.dma_start(k_scale[32 * quad : 32 * quad + 4, :].bitcast(I32), picked[rows : rows + 4, :].bitcast(I32))
-        load_q(1)
         load_q(2)
 
         nc.vector.tensor_copy(bonus_row[:], bonus_pool[:].indirect(offsets[:]))
@@ -148,8 +156,11 @@ def tile_attend_tok_ucb_srt_kernel(tc, qT, k_words, k_scales, bo, offs, out):
         quantise(1)
         quantise(2)
 
-        for c in range(len(CHUNKS)):
-            for h in range(2):
-                score(c, h)
+        score(0, 0, 2)
+        score(0, 2, 4)
+        score(1, 0, 2)
+        score(1, 2, 4)
+        score(2, 0, 2)
+        score(2, 2, 4)
         for h in range(2):
             finish(h)

@@ -72,8 +72,8 @@ def tile_attend_tok_ucb_srt_kernel(tc, qT, k_words, k_scales, bo, offs, out):
             nc.sync.dma_start(q_raw[c], q_rows[:, :, lo:hi])
 
         nc.sync.dma_start(offsets[:], offs)
-        nc.sync.dma_start(scale_pool[SCALE_ROW0:P, :].bitcast(I32), scales)
-        nc.sync.dma_start(bonus_pool[LIVE:P, :], bo[LIVE:P, :])
+        nc.scalar.dma_start(scale_pool[SCALE_ROW0:P, :].bitcast(I32), scales)
+        nc.scalar.dma_start(bonus_pool[LIVE:P, :], bo[LIVE:P, :])
         load_q(0)
         for lo, hi in ((0, PREFIX), (PREFIX, POOL)):
             nc.sync.dma_start(word_pool[:, lo:hi].bitcast(I32), words[:, lo:hi])
@@ -83,20 +83,19 @@ def tile_attend_tok_ucb_srt_kernel(tc, qT, k_words, k_scales, bo, offs, out):
         picked = sb.tile([P, SLOTS], U8, name="picked")
         k_codes = [sb.tile([P, HALF], U32, name="k_codes%d" % h, align_bytes=64) for h in range(2)]
         bonus_col = ps.tile([P, TILES, P], F32, name="bonus_col")
-        room = sb.tile([P, (NQ + UNIT) * PACK], BF16, name="room", align_bytes=64)
+        room = sb.tile([P, NQ * PACK], BF16, name="room", align_bytes=64)
         grouped = [room[:, lo * PACK : hi * PACK] for lo, hi in CHUNKS]
         q_codes = [sb.tile([P, EARLY], U32, name="q_codes0", align_bytes=64)] + [
             late.tile([P, hi - lo], U32, name="q_codes%d" % lo, align_bytes=64, offset=POOL + lo * 4)
             for lo, hi in CHUNKS[1:]
         ]
         q_scale = [sb.tile([P, hi - lo], U8, name="q_scale%d" % lo, align_bytes=64) for lo, hi in CHUNKS]
-        span = TILES * UNIT_RUNS
-        best = (
-            room[:, UNIT * PACK - span : (NQ + UNIT) * PACK - span]
-            .bitcast(F32)
-            .rearrange("p (u x) -> p u x", u=UNITS)[:, :, 0:span]
-            .rearrange("p u (r j) -> p r u j", r=TILES)
-        )
+        cells = room[:].bitcast(F32)
+        span = 2 * RUNS
+        border = CHUNKS[-1][0] * PACK // 2
+        best = [
+            cells[:, lo : lo + span].rearrange("p (u i j) -> p i u j", u=UNITS, i=2) for lo in (0, border - span // 2)
+        ]
         out_view = out[0].rearrange("(r p) j -> p r j", p=P)
 
         def score(c, first, last):
@@ -114,7 +113,7 @@ def tile_attend_tok_ucb_srt_kernel(tc, qT, k_words, k_scales, bo, offs, out):
                     stop=True,
                 )
             nc.vector.tensor_reduce(
-                best[:, first:last, lo // UNIT : hi // UNIT, :],
+                best[first // 2][:, :, lo // UNIT : hi // UNIT, :],
                 bank[:].rearrange("p i (u j s) -> p i u j s", j=UNIT_RUNS, s=SEG),
                 axis=mybir.AxisListType.X,
                 op=mybir.AluOpType.max,
@@ -125,7 +124,7 @@ def tile_attend_tok_ucb_srt_kernel(tc, qT, k_words, k_scales, bo, offs, out):
             result = sb.tile([P, 2, RUNS], F32, name="result%d" % h)
             nc.vector.tensor_tensor(
                 result[:].rearrange("p i (u j) -> p i u j", u=UNITS),
-                best[:, pair, :, :],
+                best[h],
                 bonus_col[:, pair, LIVE:P].unsqueeze(3).to_broadcast([P, 2, UNITS, UNIT_RUNS]),
                 mybir.AluOpType.add,
             )

@@ -15,17 +15,22 @@ PACK = 4
 SLOTS, POOL, D, NQ, SEG = 512, 2048, 512, 512, 16
 RUNS = NQ // SEG
 TILES = SLOTS // P
-HALF = SLOTS // 2
+PAIR = 2
+HALF = PAIR * P
 LIST_ROWS = 16
-QUADRANTS = 4
+QUADRANTS, QUADRANT, SCALE_ROWS = 4, 32, 4
 PREFIX = POOL - HALF
 LIVE = P - 1
 SCALE_ROW0 = P - D // 32
-CHUNKS = ((0, 256), (256, 384), (384, 512))
-EARLY = CHUNKS[0][1]
+PARTS = ((0, 256), (256, 384), (384, 512))
+EARLY = PARTS[0][1]
 UNIT = 128
 UNITS = NQ // UNIT
 UNIT_RUNS = UNIT // SEG
+
+SCALES_AT = 0
+WORDS_AT = SCALES_AT + POOL
+EARLY_AT = WORDS_AT + POOL * 4
 
 FLOPS = 2 * SLOTS * D * NQ
 BYTES = D * NQ * 4 + P * POOL * 4 + (D // 32) * POOL + POOL * 4 + P * (SLOTS // LIST_ROWS) * 2 + SLOTS * RUNS * 4
@@ -35,12 +40,12 @@ def tile_attend_tok_ucb_srt_kernel(tc, qT, k_words, k_scales, bo, offs, out):
     nc = tc.nc
     with ExitStack() as ctx:
         sb = ctx.enter_context(tc.tile_pool(name="sb", bufs=1))
-        late = ctx.enter_context(tc.tile_pool(name="late", bufs=1))
+        shared = ctx.enter_context(tc.tile_pool(name="shared", bufs=1))
         ps = ctx.enter_context(tc.psum_pool(name="ps", bufs=1))
 
         offsets = sb.tile([P, SLOTS // LIST_ROWS], U16, name="offsets")
         bonus_pool = sb.tile([P, POOL], F32, name="bonus_pool")
-        scale_pool = late.tile([P, POOL], U8, name="scale_pool", offset=0)
+        scale_pool = shared.tile([P, POOL], U8, name="scale_pool", offset=SCALES_AT)
         k_scale = sb.tile([P, SLOTS], U8, name="k_scale", align_bytes=64)
         ident = sb.tile([P, P], F32, name="ident")
 
@@ -58,9 +63,9 @@ def tile_attend_tok_ucb_srt_kernel(tc, qT, k_words, k_scales, bo, offs, out):
             pattern=[[-1, P]],
             channel_multiplier=1,
         )
-        word_pool = late.tile([P, POOL], U32, name="word_pool", offset=POOL)
-        q_tiles = [sb.tile([P, PACK * (hi - lo)], F32, name="q_raw%d" % lo) for lo, hi in CHUNKS[:-1]]
-        q_tiles.append(late.tile([P, PACK * (NQ - CHUNKS[-1][0])], F32, name="q_last", offset=0))
+        word_pool = shared.tile([P, POOL], U32, name="word_pool", offset=WORDS_AT)
+        q_tiles = [sb.tile([P, PACK * (hi - lo)], F32, name="q_raw%d" % lo) for lo, hi in PARTS[:-1]]
+        q_tiles.append(shared.tile([P, PACK * (NQ - PARTS[-1][0])], F32, name="q_last", offset=SCALES_AT))
         q_raw = [t[:].rearrange("p (t w) -> p t w", t=PACK) for t in q_tiles]
 
         q_rows = qT[0].rearrange("(p t) w -> p t w", t=PACK)
@@ -68,7 +73,7 @@ def tile_attend_tok_ucb_srt_kernel(tc, qT, k_words, k_scales, bo, offs, out):
         scales = k_scales[0].bitcast(I32)
 
         def load_q(c):
-            lo, hi = CHUNKS[c]
+            lo, hi = PARTS[c]
             nc.sync.dma_start(q_raw[c], q_rows[:, :, lo:hi])
 
         nc.sync.dma_start(offsets[:], offs)
@@ -81,30 +86,38 @@ def tile_attend_tok_ucb_srt_kernel(tc, qT, k_words, k_scales, bo, offs, out):
 
         bonus_row = sb.tile([P, SLOTS], F32, name="bonus_row")
         picked = sb.tile([P, SLOTS], U8, name="picked")
-        k_codes = [sb.tile([P, HALF], U32, name="k_codes%d" % h, align_bytes=64) for h in range(2)]
-        bonus_col = ps.tile([P, TILES, P], F32, name="bonus_col")
-        room = sb.tile([P, NQ * PACK], BF16, name="room", align_bytes=64)
-        grouped = [room[:, lo * PACK : hi * PACK] for lo, hi in CHUNKS]
-        q_codes = [sb.tile([P, EARLY], U32, name="q_codes0", align_bytes=64)] + [
-            late.tile([P, hi - lo], U32, name="q_codes%d" % lo, align_bytes=64, offset=POOL + lo * 4)
-            for lo, hi in CHUNKS[1:]
+        grouped_early = shared.tile([P, EARLY * PACK], BF16, name="grouped_early", align_bytes=64, offset=EARLY_AT)
+        k_codes = [
+            shared.tile([P, HALF], U32, name="k_codes%d" % h, align_bytes=64, offset=EARLY_AT + h * HALF * 4)
+            for h in range(2)
         ]
-        q_scale = [sb.tile([P, hi - lo], U8, name="q_scale%d" % lo, align_bytes=64) for lo, hi in CHUNKS]
-        cells = room[:].bitcast(F32)
-        span = 2 * RUNS
-        border = CHUNKS[-1][0] * PACK // 2
+        bonus_col = ps.tile([P, TILES, P], F32, name="bonus_col")
+        grouped_late = sb.tile([P, (NQ - EARLY) * PACK], BF16, name="grouped_late", align_bytes=64)
+        grouped = [grouped_early[:]] + [
+            grouped_late[:, (lo - EARLY) * PACK : (hi - EARLY) * PACK] for lo, hi in PARTS[1:]
+        ]
+        q_codes = [sb.tile([P, EARLY], U32, name="q_codes0", align_bytes=64)] + [
+            shared.tile([P, hi - lo], U32, name="q_codes%d" % lo, align_bytes=64, offset=WORDS_AT + lo * 4)
+            for lo, hi in PARTS[1:]
+        ]
+        q_scale = [sb.tile([P, hi - lo], U8, name="q_scale%d" % lo, align_bytes=64) for lo, hi in PARTS]
+        late_cells = grouped_late[:].bitcast(F32)
+        span = PAIR * RUNS
+        border = (PARTS[-1][0] - EARLY) * PACK // 2
+        best_first = sb.tile([P, span], F32, name="best_first")
         best = [
-            cells[:, lo : lo + span].rearrange("p (u i j) -> p i u j", u=UNITS, i=2) for lo in (0, border - span // 2)
+            t.rearrange("p (u i j) -> p i u j", u=UNITS, i=PAIR)
+            for t in (best_first[:], late_cells[:, border - span // 2 : border + span // 2])
         ]
         out_view = out[0].rearrange("(r p) j -> p r j", p=P)
 
-        def score(c, first, last):
-            lo, hi = CHUNKS[c]
-            bank = ps.tile([P, last - first, hi - lo], F32, name="scores%d_%d" % (c, first))
-            for r in range(first, last):
-                h, i = divmod(r, 2)
+        def score(c, h):
+            lo, hi = PARTS[c]
+            bank = ps.tile([P, PAIR, hi - lo], F32, name="scores%d_%d" % (c, h))
+            for i in range(PAIR):
+                r = PAIR * h + i
                 nc.tensor.matmul_mx(
-                    out=bank[:, r - first, :],
+                    out=bank[:, i, :],
                     lhsT=k_codes[h][:, i * P : (i + 1) * P].bitcast(FP8X4),
                     lhsT_scale=k_scale[:, r * P : (r + 1) * P],
                     rhs=q_codes[c][:].bitcast(FP8X4),
@@ -113,34 +126,36 @@ def tile_attend_tok_ucb_srt_kernel(tc, qT, k_words, k_scales, bo, offs, out):
                     stop=True,
                 )
             nc.vector.tensor_reduce(
-                best[first // 2][:, :, lo // UNIT : hi // UNIT, :],
+                best[h][:, :, lo // UNIT : hi // UNIT, :],
                 bank[:].rearrange("p i (u j s) -> p i u j s", j=UNIT_RUNS, s=SEG),
                 axis=mybir.AxisListType.X,
                 op=mybir.AluOpType.max,
             )
 
         def finish(h):
-            pair = slice(2 * h, 2 * h + 2)
-            result = sb.tile([P, 2, RUNS], F32, name="result%d" % h)
+            pair = slice(PAIR * h, PAIR * (h + 1))
+            result = sb.tile([P, PAIR, RUNS], F32, name="result%d" % h)
             nc.vector.tensor_tensor(
                 result[:].rearrange("p i (u j) -> p i u j", u=UNITS),
                 best[h],
-                bonus_col[:, pair, LIVE:P].unsqueeze(3).to_broadcast([P, 2, UNITS, UNIT_RUNS]),
+                bonus_col[:, pair, LIVE:P].unsqueeze(3).to_broadcast([P, PAIR, UNITS, UNIT_RUNS]),
                 mybir.AluOpType.add,
             )
             nc.sync.dma_start(out_view[:, pair, :], result[:])
 
         nc.vector.tensor_copy(picked[:], scale_pool[:].indirect(offsets[:]))
         for quad in range(QUADRANTS):
-            rows = SCALE_ROW0 + 4 * quad
-            nc.sync.dma_start(k_scale[32 * quad : 32 * quad + 4, :].bitcast(I32), picked[rows : rows + 4, :].bitcast(I32))
+            src, dst = SCALE_ROW0 + SCALE_ROWS * quad, QUADRANT * quad
+            nc.sync.dma_start(
+                k_scale[dst : dst + SCALE_ROWS, :].bitcast(I32), picked[src : src + SCALE_ROWS, :].bitcast(I32)
+            )
         load_q(2)
 
         nc.vector.tensor_copy(bonus_row[:], bonus_pool[:].indirect(offsets[:]))
         for r in range(TILES):
             nc.tensor.transpose(bonus_col[:, r, :], bonus_row[:, r * P : (r + 1) * P], ident[:])
 
-        for c in range(len(CHUNKS)):
+        for c in range(len(PARTS)):
             nc.scalar.copy(
                 grouped[c].rearrange("p (w i t) -> p w t i", i=4, t=PACK),
                 q_raw[c].rearrange("p t (w i) -> p w t i", i=4),
@@ -155,11 +170,8 @@ def tile_attend_tok_ucb_srt_kernel(tc, qT, k_words, k_scales, bo, offs, out):
         quantise(1)
         quantise(2)
 
-        score(0, 0, 2)
-        score(0, 2, 4)
-        score(1, 0, 2)
-        score(1, 2, 4)
-        score(2, 0, 2)
-        score(2, 2, 4)
+        for c in range(len(PARTS)):
+            for h in range(2):
+                score(c, h)
         for h in range(2):
             finish(h)

@@ -28,8 +28,12 @@ UNIT = 128
 UNITS = NQ // UNIT
 UNIT_RUNS = UNIT // SEG
 
-SCALES_AT = 0
-WORDS_AT = SCALES_AT + POOL
+LAP = 64
+RAW_BYTES = PACK * UNIT * 4
+SCALES_AT = RAW_BYTES - LAP
+PLANE_AT = RAW_BYTES
+LAST_AT = SCALES_AT + POOL - LAP
+WORDS_AT = LAST_AT + RAW_BYTES
 EARLY_AT = WORDS_AT + POOL * 4
 
 FLOPS = 2 * SLOTS * D * NQ
@@ -46,14 +50,12 @@ def tile_attend_tok_ucb_srt_kernel(tc, qT, k_words, k_scales, bo, offs, out):
         offsets = sb.tile([P, SLOTS // LIST_ROWS], U16, name="offsets")
         bonus_pool = sb.tile([P, POOL], F32, name="bonus_pool")
         scale_pool = shared.tile([P, POOL], U8, name="scale_pool", offset=SCALES_AT)
-        k_scale = sb.tile([P, SLOTS], U8, name="k_scale", align_bytes=64)
         ident = sb.tile([P, P], F32, name="ident")
 
         zeros = sb.tile([P, P], F32, name="zeros")
+        nc.vector.memset(zeros[:], 0.0)
         nc.vector.memset(scale_pool[0:SCALE_ROW0, :].bitcast(I32), 0)
         nc.vector.memset(bonus_pool[0:LIVE, :], 0.0)
-        nc.gpsimd.memset(k_scale[:].bitcast(I32), 0)
-        nc.gpsimd.memset(zeros[:], 0.0)
         nc.gpsimd.affine_select(
             out=ident[:],
             in_=zeros[:],
@@ -64,8 +66,9 @@ def tile_attend_tok_ucb_srt_kernel(tc, qT, k_words, k_scales, bo, offs, out):
             channel_multiplier=1,
         )
         word_pool = shared.tile([P, POOL], U32, name="word_pool", offset=WORDS_AT)
-        q_tiles = [sb.tile([P, PACK * (hi - lo)], F32, name="q_raw%d" % lo) for lo, hi in PARTS[:-1]]
-        q_tiles.append(shared.tile([P, PACK * (NQ - PARTS[-1][0])], F32, name="q_last", offset=SCALES_AT))
+        q_tiles = [sb.tile([P, PACK * EARLY], F32, name="q_early")] + [
+            shared.tile([P, PACK * UNIT], F32, name="q_late%d" % at, offset=at) for at in (0, LAST_AT)
+        ]
         q_raw = [t[:].rearrange("p (t w) -> p t w", t=PACK) for t in q_tiles]
 
         q_rows = qT[0].rearrange("(p t) w -> p t w", t=PACK)
@@ -77,12 +80,11 @@ def tile_attend_tok_ucb_srt_kernel(tc, qT, k_words, k_scales, bo, offs, out):
             nc.sync.dma_start(q_raw[c], q_rows[:, :, lo:hi])
 
         nc.sync.dma_start(offsets[:], offs)
-        nc.scalar.dma_start(scale_pool[SCALE_ROW0:P, :].bitcast(I32), scales)
+        nc.sync.dma_start(scale_pool[SCALE_ROW0:P, :].bitcast(I32), scales)
         nc.scalar.dma_start(bonus_pool[LIVE:P, :], bo[LIVE:P, :])
         load_q(0)
         for lo, hi in ((0, PREFIX), (PREFIX, POOL)):
             nc.sync.dma_start(word_pool[:, lo:hi].bitcast(I32), words[:, lo:hi])
-        load_q(1)
 
         bonus_row = sb.tile([P, SLOTS], F32, name="bonus_row")
         picked = sb.tile([P, SLOTS], U8, name="picked")
@@ -111,13 +113,13 @@ def tile_attend_tok_ucb_srt_kernel(tc, qT, k_words, k_scales, bo, offs, out):
         ]
         out_view = out[0].rearrange("(r p) j -> p r j", p=P)
 
-        def score(c, h):
+        def score(c, h, tiles):
             lo, hi = PARTS[c]
-            bank = ps.tile([P, PAIR, hi - lo], F32, name="scores%d_%d" % (c, h))
-            for i in range(PAIR):
+            bank = ps.tile([P, len(tiles), hi - lo], F32, name="scores%d_%d_%d" % (c, h, tiles[0]))
+            for n, i in enumerate(tiles):
                 r = PAIR * h + i
                 nc.tensor.matmul_mx(
-                    out=bank[:, i, :],
+                    out=bank[:, n, :],
                     lhsT=k_codes[h][:, i * P : (i + 1) * P].bitcast(FP8X4),
                     lhsT_scale=k_scale[:, r * P : (r + 1) * P],
                     rhs=q_codes[c][:].bitcast(FP8X4),
@@ -126,7 +128,7 @@ def tile_attend_tok_ucb_srt_kernel(tc, qT, k_words, k_scales, bo, offs, out):
                     stop=True,
                 )
             nc.vector.tensor_reduce(
-                best[h][:, :, lo // UNIT : hi // UNIT, :],
+                best[h][:, tiles[0] : tiles[-1] + 1, lo // UNIT : hi // UNIT, :],
                 bank[:].rearrange("p i (u j s) -> p i u j s", j=UNIT_RUNS, s=SEG),
                 axis=mybir.AxisListType.X,
                 op=mybir.AluOpType.max,
@@ -144,11 +146,13 @@ def tile_attend_tok_ucb_srt_kernel(tc, qT, k_words, k_scales, bo, offs, out):
             nc.sync.dma_start(out_view[:, pair, :], result[:])
 
         nc.vector.tensor_copy(picked[:], scale_pool[:].indirect(offsets[:]))
+        k_scale = shared.tile([P, SLOTS], U8, name="k_scale", align_bytes=64, offset=PLANE_AT)
         for quad in range(QUADRANTS):
             src, dst = SCALE_ROW0 + SCALE_ROWS * quad, QUADRANT * quad
             nc.sync.dma_start(
                 k_scale[dst : dst + SCALE_ROWS, :].bitcast(I32), picked[src : src + SCALE_ROWS, :].bitcast(I32)
             )
+        load_q(1)
         load_q(2)
 
         nc.vector.tensor_copy(bonus_row[:], bonus_pool[:].indirect(offsets[:]))
@@ -172,6 +176,7 @@ def tile_attend_tok_ucb_srt_kernel(tc, qT, k_words, k_scales, bo, offs, out):
 
         for c in range(len(PARTS)):
             for h in range(2):
-                score(c, h)
+                for tiles in ((0,), (1,)) if (c, h) == (0, 0) else ((0, 1),):
+                    score(c, h, tiles)
         for h in range(2):
             finish(h)

@@ -35,6 +35,9 @@ PLANE_AT = RAW_BYTES
 LAST_AT = SCALES_AT + POOL - LAP
 WORDS_AT = LAST_AT + RAW_BYTES
 EARLY_AT = WORDS_AT + POOL * 4
+BONUS_AT = EARLY_AT + SLOTS * 4
+FIRST_AT = BONUS_AT + POOL * 4
+IDENT_AT = FIRST_AT - P * 2
 
 FLOPS = 2 * SLOTS * D * NQ
 BYTES = D * NQ * 4 + P * POOL * 4 + (D // 32) * POOL + POOL * 4 + P * (SLOTS // LIST_ROWS) * 2 + SLOTS * RUNS * 4
@@ -48,17 +51,16 @@ def tile_attend_tok_ucb_srt_kernel(tc, qT, k_words, k_scales, bo, offs, out):
         ps = ctx.enter_context(tc.psum_pool(name="ps", bufs=1))
 
         offsets = sb.tile([P, SLOTS // LIST_ROWS], U16, name="offsets")
-        bonus_pool = sb.tile([P, POOL], F32, name="bonus_pool")
+        bonus_pool = shared.tile([P, POOL], F32, name="bonus_pool", offset=BONUS_AT)
         scale_pool = shared.tile([P, POOL], U8, name="scale_pool", offset=SCALES_AT)
-        ident = sb.tile([P, P], F32, name="ident")
 
-        zeros = sb.tile([P, P], F32, name="zeros")
-        nc.vector.memset(zeros[:], 0.0)
+        narrow = sb.tile([P, P], BF16, name="narrow")
+        nc.vector.memset(narrow[:], 0.0)
         nc.vector.memset(scale_pool[0:SCALE_ROW0, :].bitcast(I32), 0)
         nc.vector.memset(bonus_pool[0:LIVE, :], 0.0)
         nc.gpsimd.affine_select(
-            out=ident[:],
-            in_=zeros[:],
+            out=narrow[:],
+            in_=narrow[:],
             compare_op=mybir.AluOpType.not_equal,
             fill=1.0,
             base=0,
@@ -66,7 +68,7 @@ def tile_attend_tok_ucb_srt_kernel(tc, qT, k_words, k_scales, bo, offs, out):
             channel_multiplier=1,
         )
         word_pool = shared.tile([P, POOL], U32, name="word_pool", offset=WORDS_AT)
-        q_tiles = [sb.tile([P, PACK * EARLY], F32, name="q_early")] + [
+        q_tiles = [shared.tile([P, PACK * EARLY], F32, name="q_early", offset=FIRST_AT)] + [
             shared.tile([P, PACK * UNIT], F32, name="q_late%d" % at, offset=at) for at in (0, LAST_AT)
         ]
         q_raw = [t[:].rearrange("p (t w) -> p t w", t=PACK) for t in q_tiles]
@@ -103,14 +105,10 @@ def tile_attend_tok_ucb_srt_kernel(tc, qT, k_words, k_scales, bo, offs, out):
             for lo, hi in PARTS[1:]
         ]
         q_scale = [sb.tile([P, hi - lo], U8, name="q_scale%d" % lo, align_bytes=64) for lo, hi in PARTS]
-        late_cells = grouped_late[:].bitcast(F32)
         span = PAIR * RUNS
-        border = (PARTS[-1][0] - EARLY) * PACK // 2
         best_first = sb.tile([P, span], F32, name="best_first")
-        best = [
-            t.rearrange("p (u i j) -> p i u j", u=UNITS, i=PAIR)
-            for t in (best_first[:], late_cells[:, border - span // 2 : border + span // 2])
-        ]
+        best_second = shared.tile([P, span], F32, name="best_second", offset=0)
+        best = [t[:].rearrange("p (u i j) -> p i u j", u=UNITS, i=PAIR) for t in (best_first, best_second)]
         out_view = out[0].rearrange("(r p) j -> p r j", p=P)
 
         def score(c, h, tiles):
@@ -156,14 +154,20 @@ def tile_attend_tok_ucb_srt_kernel(tc, qT, k_words, k_scales, bo, offs, out):
         load_q(2)
 
         nc.vector.tensor_copy(bonus_row[:], bonus_pool[:].indirect(offsets[:]))
-        for r in range(TILES):
-            nc.tensor.transpose(bonus_col[:, r, :], bonus_row[:, r * P : (r + 1) * P], ident[:])
 
-        for c in range(len(PARTS)):
+        def interleave(c):
             nc.scalar.copy(
                 grouped[c].rearrange("p (w i t) -> p w t i", i=4, t=PACK),
                 q_raw[c].rearrange("p t (w i) -> p w t i", i=4),
             )
+
+        interleave(0)
+        ident = shared.tile([P, P], F32, name="ident", offset=IDENT_AT)
+        nc.scalar.copy(ident[:], narrow[:])
+        for r in range(TILES):
+            nc.tensor.transpose(bonus_col[:, r, :], bonus_row[:, r * P : (r + 1) * P], ident[:])
+        interleave(1)
+        interleave(2)
 
         def quantise(c):
             nc.vector.quantize_mx(out=q_codes[c][:].bitcast(FP8X4), scales=q_scale[c][:], in_=grouped[c])
@@ -171,12 +175,13 @@ def tile_attend_tok_ucb_srt_kernel(tc, qT, k_words, k_scales, bo, offs, out):
         quantise(0)
         nc.vector.tensor_copy(k_codes[0][:], word_pool[:, 0:PREFIX].indirect(offsets[:, 0 : HALF // LIST_ROWS]))
         nc.vector.tensor_copy(k_codes[1][:], word_pool[:].indirect(offsets[:, HALF // LIST_ROWS :]))
+        score(0, 0, (0,))
+        score(0, 0, (1,))
         quantise(1)
+        score(0, 1, (0, 1))
         quantise(2)
-
-        for c in range(len(PARTS)):
+        for c in range(1, len(PARTS)):
             for h in range(2):
-                for tiles in ((0,), (1,)) if (c, h) == (0, 0) else ((0, 1),):
-                    score(c, h, tiles)
+                score(c, h, (0, 1))
         for h in range(2):
             finish(h)

@@ -105,43 +105,38 @@ def tile_attend_tok_ucb_srt_kernel(tc, qT, k_words, k_scales, bo, offs, out):
             for lo, hi in PARTS[1:]
         ]
         q_scale = [sb.tile([P, hi - lo], U8, name="q_scale%d" % lo, align_bytes=64) for lo, hi in PARTS]
-        span = PAIR * RUNS
-        best_first = sb.tile([P, span], F32, name="best_first")
-        best_second = shared.tile([P, span], F32, name="best_second", offset=0)
-        best = [t[:].rearrange("p (u i j) -> p i u j", u=UNITS, i=PAIR) for t in (best_first, best_second)]
+        cells = PAIR * UNIT_RUNS
+        best_first = sb.tile([P, UNITS * cells], F32, name="best_first")
+        best_mid = shared.tile([P, cells], F32, name="best_mid", offset=0)
+        best_late = shared.tile([P, 2 * cells], F32, name="best_late", offset=LAST_AT + RAW_BYTES - 2 * cells * 4)
+        first, mid, late = (
+            t[:].rearrange("p (u i j) -> p i u j", i=PAIR, j=UNIT_RUNS) for t in (best_first, best_mid, best_late)
+        )
         out_view = out[0].rearrange("(r p) j -> p r j", p=P)
 
-        def score(c, h, tiles):
-            lo, hi = PARTS[c]
-            bank = ps.tile([P, len(tiles), hi - lo], F32, name="scores%d_%d_%d" % (c, h, tiles[0]))
+        def multiply(c, h, tiles, lo, hi, tag):
+            bank = ps.tile([P, len(tiles), hi - lo], F32, name="scores", tag=tag)
+            rows = slice(lo - PARTS[c][0], hi - PARTS[c][0])
             for n, i in enumerate(tiles):
                 r = PAIR * h + i
                 nc.tensor.matmul_mx(
                     out=bank[:, n, :],
                     lhsT=k_codes[h][:, i * P : (i + 1) * P].bitcast(FP8X4),
                     lhsT_scale=k_scale[:, r * P : (r + 1) * P],
-                    rhs=q_codes[c][:].bitcast(FP8X4),
-                    rhs_scale=q_scale[c][:],
+                    rhs=q_codes[c][:, rows].bitcast(FP8X4),
+                    rhs_scale=q_scale[c][:, rows],
                     start=True,
                     stop=True,
                 )
+            return bank
+
+        def reduce(target, scores):
             nc.vector.tensor_reduce(
-                best[h][:, tiles[0] : tiles[-1] + 1, lo // UNIT : hi // UNIT, :],
-                bank[:].rearrange("p i (u j s) -> p i u j s", j=UNIT_RUNS, s=SEG),
+                target,
+                scores.rearrange("p i (u j s) -> p i u j s", j=UNIT_RUNS, s=SEG),
                 axis=mybir.AxisListType.X,
                 op=mybir.AluOpType.max,
             )
-
-        def finish(h):
-            pair = slice(PAIR * h, PAIR * (h + 1))
-            result = sb.tile([P, PAIR, RUNS], F32, name="result%d" % h)
-            nc.vector.tensor_tensor(
-                result[:].rearrange("p i (u j) -> p i u j", u=UNITS),
-                best[h],
-                bonus_col[:, pair, LIVE:P].unsqueeze(3).to_broadcast([P, PAIR, UNITS, UNIT_RUNS]),
-                mybir.AluOpType.add,
-            )
-            nc.sync.dma_start(out_view[:, pair, :], result[:])
 
         nc.vector.tensor_copy(picked[:], scale_pool[:].indirect(offsets[:]))
         k_scale = shared.tile([P, SLOTS], U8, name="k_scale", align_bytes=64, offset=PLANE_AT)
@@ -175,13 +170,38 @@ def tile_attend_tok_ucb_srt_kernel(tc, qT, k_words, k_scales, bo, offs, out):
         quantise(0)
         nc.vector.tensor_copy(k_codes[0][:], word_pool[:, 0:PREFIX].indirect(offsets[:, 0 : HALF // LIST_ROWS]))
         nc.vector.tensor_copy(k_codes[1][:], word_pool[:].indirect(offsets[:, HALF // LIST_ROWS :]))
-        score(0, 0, (0,))
-        score(0, 0, (1,))
+        both = (0, 1)
+        for i in range(PAIR):
+            reduce(first[:, i : i + 1, 0:2, :], multiply(0, 0, (i,), 0, EARLY, "bank%d" % i)[:])
         quantise(1)
-        score(0, 1, (0, 1))
+        reduce(mid, multiply(0, 1, both, UNIT, EARLY, "bank2")[:])
+        held = multiply(0, 1, both, 0, UNIT, "bank3")
         quantise(2)
-        for c in range(1, len(PARTS)):
-            for h in range(2):
-                score(c, h, (0, 1))
-        for h in range(2):
-            finish(h)
+        shifted = shared.tile([P, PAIR * UNIT + TILES], F32, name="shifted", offset=LAST_AT)
+        bonus = shifted[:, PAIR * UNIT :]
+        nc.scalar.copy(bonus, bonus_col[:, :, LIVE])
+
+        def add_on_scalar(target, source, r):
+            nc.scalar.activation(target, source, mybir.ActivationFunctionType.Identity, bias=bonus[:, r : r + 1])
+
+        for i in range(PAIR):
+            add_on_scalar(shifted[:, i * UNIT : (i + 1) * UNIT], held[:, i, :], PAIR + i)
+        for c, h, tag in ((1, 1, "bank4"), (1, 0, "bank5"), (2, 0, "bank6"), (2, 1, "bank0")):
+            target = late[:, :, c - 1 : c, :] if h else first[:, :, c + 1 : c + 2, :]
+            reduce(target, multiply(c, h, both, PARTS[c][0], PARTS[c][1], tag)[:])
+        result_first = sb.tile([P, PAIR, RUNS], F32, name="result_first")
+        result_second = shared.tile([P, PAIR, RUNS], F32, name="result_second", offset=WORDS_AT + PARTS[2][0] * 4)
+        by_unit = [t[:].rearrange("p i (u j) -> p i u j", u=UNITS) for t in (result_first, result_second)]
+        for i in range(PAIR):
+            add_on_scalar(by_unit[1][:, i, 1, :], mid[:, i, 0, :], PAIR + i)
+        for i in range(PAIR):
+            add_on_scalar(by_unit[0][:, i, :, :], first[:, i, :, :], i)
+        nc.sync.dma_start(out_view[:, 0:PAIR, :], result_first[:])
+        reduce(by_unit[1][:, :, 0:1, :], shifted[:, 0 : PAIR * UNIT].rearrange("p (i w) -> p i w", i=PAIR))
+        nc.vector.tensor_tensor(
+            by_unit[1][:, :, 2:UNITS, :],
+            late,
+            bonus_col[:, PAIR:TILES, LIVE:P].unsqueeze(3).to_broadcast([P, PAIR, 2, UNIT_RUNS]),
+            mybir.AluOpType.add,
+        )
+        nc.sync.dma_start(out_view[:, PAIR:TILES, :], result_second[:])

@@ -22,22 +22,23 @@ QUADRANTS, QUADRANT, SCALE_ROWS = 4, 32, 4
 PREFIX = POOL - HALF
 LIVE = P - 1
 SCALE_ROW0 = P - D // 32
-PARTS = ((0, 256), (256, 384), (384, 512))
-EARLY = PARTS[0][1]
 UNIT = 128
 UNITS = NQ // UNIT
 UNIT_RUNS = UNIT // SEG
+PARTS = ((0, 2 * UNIT), (2 * UNIT, 3 * UNIT), (3 * UNIT, NQ))
+EARLY = PARTS[0][1]
 
 LAP = 64
 RAW_BYTES = PACK * UNIT * 4
+MID_AT = 0
 SCALES_AT = RAW_BYTES - LAP
 PLANE_AT = RAW_BYTES
 LAST_AT = SCALES_AT + POOL - LAP
 WORDS_AT = LAST_AT + RAW_BYTES
-EARLY_AT = WORDS_AT + POOL * 4
-BONUS_AT = EARLY_AT + SLOTS * 4
+BONUS_AT = WORDS_AT + POOL * 4
 FIRST_AT = BONUS_AT + POOL * 4
 IDENT_AT = FIRST_AT - P * 2
+CODES_AT = FIRST_AT + P * 2
 
 FLOPS = 2 * SLOTS * D * NQ
 BYTES = D * NQ * 4 + P * POOL * 4 + (D // 32) * POOL + POOL * 4 + P * (SLOTS // LIST_ROWS) * 2 + SLOTS * RUNS * 4
@@ -54,13 +55,13 @@ def tile_attend_tok_ucb_srt_kernel(tc, qT, k_words, k_scales, bo, offs, out):
         bonus_pool = shared.tile([P, POOL], F32, name="bonus_pool", offset=BONUS_AT)
         scale_pool = shared.tile([P, POOL], U8, name="scale_pool", offset=SCALES_AT)
 
-        narrow = sb.tile([P, P], BF16, name="narrow")
-        nc.vector.memset(narrow[:], 0.0)
+        ident_narrow = sb.tile([P, P], BF16, name="ident_narrow")
+        nc.vector.memset(ident_narrow[:], 0.0)
         nc.vector.memset(scale_pool[0:SCALE_ROW0, :].bitcast(I32), 0)
         nc.vector.memset(bonus_pool[0:LIVE, :], 0.0)
         nc.gpsimd.affine_select(
-            out=narrow[:],
-            in_=narrow[:],
+            out=ident_narrow[:],
+            in_=ident_narrow[:],
             compare_op=mybir.AluOpType.not_equal,
             fill=1.0,
             base=0,
@@ -69,7 +70,7 @@ def tile_attend_tok_ucb_srt_kernel(tc, qT, k_words, k_scales, bo, offs, out):
         )
         word_pool = shared.tile([P, POOL], U32, name="word_pool", offset=WORDS_AT)
         q_tiles = [shared.tile([P, PACK * EARLY], F32, name="q_early", offset=FIRST_AT)] + [
-            shared.tile([P, PACK * UNIT], F32, name="q_late%d" % at, offset=at) for at in (0, LAST_AT)
+            shared.tile([P, PACK * UNIT], F32, name="q_late%d" % at, offset=at) for at in (MID_AT, LAST_AT)
         ]
         q_raw = [t[:].rearrange("p (t w) -> p t w", t=PACK) for t in q_tiles]
 
@@ -90,9 +91,9 @@ def tile_attend_tok_ucb_srt_kernel(tc, qT, k_words, k_scales, bo, offs, out):
 
         bonus_row = sb.tile([P, SLOTS], F32, name="bonus_row")
         picked = sb.tile([P, SLOTS], U8, name="picked")
-        grouped_early = shared.tile([P, EARLY * PACK], BF16, name="grouped_early", align_bytes=64, offset=EARLY_AT)
+        grouped_early = sb.tile([P, EARLY * PACK], BF16, name="grouped_early", align_bytes=64)
         k_codes = [
-            shared.tile([P, HALF], U32, name="k_codes%d" % h, align_bytes=64, offset=EARLY_AT + h * HALF * 4)
+            shared.tile([P, HALF], U32, name="k_codes%d" % h, align_bytes=64, offset=CODES_AT + h * HALF * 4)
             for h in range(2)
         ]
         bonus_col = ps.tile([P, TILES, P], F32, name="bonus_col")
@@ -107,15 +108,15 @@ def tile_attend_tok_ucb_srt_kernel(tc, qT, k_words, k_scales, bo, offs, out):
         q_scale = [sb.tile([P, hi - lo], U8, name="q_scale%d" % lo, align_bytes=64) for lo, hi in PARTS]
         cells = PAIR * UNIT_RUNS
         best_first = sb.tile([P, UNITS * cells], F32, name="best_first")
-        best_mid = shared.tile([P, cells], F32, name="best_mid", offset=0)
+        best_mid = shared.tile([P, cells], F32, name="best_mid", offset=MID_AT)
         best_late = shared.tile([P, 2 * cells], F32, name="best_late", offset=LAST_AT + RAW_BYTES - 2 * cells * 4)
         first, mid, late = (
             t[:].rearrange("p (u i j) -> p i u j", i=PAIR, j=UNIT_RUNS) for t in (best_first, best_mid, best_late)
         )
         out_view = out[0].rearrange("(r p) j -> p r j", p=P)
 
-        def multiply(c, h, tiles, lo, hi, tag):
-            bank = ps.tile([P, len(tiles), hi - lo], F32, name="scores", tag=tag)
+        def multiply(c, h, tiles, lo, hi, bank_tag):
+            bank = ps.tile([P, len(tiles), hi - lo], F32, name="scores", tag=bank_tag)
             rows = slice(lo - PARTS[c][0], hi - PARTS[c][0])
             for n, i in enumerate(tiles):
                 r = PAIR * h + i
@@ -158,7 +159,7 @@ def tile_attend_tok_ucb_srt_kernel(tc, qT, k_words, k_scales, bo, offs, out):
 
         interleave(0)
         ident = shared.tile([P, P], F32, name="ident", offset=IDENT_AT)
-        nc.scalar.copy(ident[:], narrow[:])
+        nc.scalar.copy(ident[:], ident_narrow[:])
         for r in range(TILES):
             nc.tensor.transpose(bonus_col[:, r, :], bonus_row[:, r * P : (r + 1) * P], ident[:])
         interleave(1)
@@ -172,10 +173,12 @@ def tile_attend_tok_ucb_srt_kernel(tc, qT, k_words, k_scales, bo, offs, out):
         nc.vector.tensor_copy(k_codes[1][:], word_pool[:].indirect(offsets[:, HALF // LIST_ROWS :]))
         both = (0, 1)
         for i in range(PAIR):
-            reduce(first[:, i : i + 1, 0:2, :], multiply(0, 0, (i,), 0, EARLY, "bank%d" % i)[:])
+            for u in range(EARLY // UNIT):
+                scores = multiply(0, 0, (i,), u * UNIT, (u + 1) * UNIT, "bank%d" % (2 * i + u))
+                reduce(first[:, i : i + 1, u : u + 1, :], scores[:])
         quantise(1)
-        reduce(mid, multiply(0, 1, both, UNIT, EARLY, "bank2")[:])
-        held = multiply(0, 1, both, 0, UNIT, "bank3")
+        reduce(mid, multiply(0, 1, both, UNIT, EARLY, "bank4")[:])
+        held = multiply(0, 1, both, 0, UNIT, "bank5")
         quantise(2)
         shifted = shared.tile([P, PAIR * UNIT + TILES], F32, name="shifted", offset=LAST_AT)
         bonus = shifted[:, PAIR * UNIT :]
@@ -186,9 +189,9 @@ def tile_attend_tok_ucb_srt_kernel(tc, qT, k_words, k_scales, bo, offs, out):
 
         for i in range(PAIR):
             add_on_scalar(shifted[:, i * UNIT : (i + 1) * UNIT], held[:, i, :], PAIR + i)
-        for c, h, tag in ((1, 1, "bank4"), (1, 0, "bank5"), (2, 0, "bank6"), (2, 1, "bank0")):
+        for c, h, bank_tag in ((1, 1, "bank6"), (1, 0, "bank0"), (2, 0, "bank1"), (2, 1, "bank2")):
             target = late[:, :, c - 1 : c, :] if h else first[:, :, c + 1 : c + 2, :]
-            reduce(target, multiply(c, h, both, PARTS[c][0], PARTS[c][1], tag)[:])
+            reduce(target, multiply(c, h, both, PARTS[c][0], PARTS[c][1], bank_tag)[:])
         result_first = sb.tile([P, PAIR, RUNS], F32, name="result_first")
         result_second = shared.tile([P, PAIR, RUNS], F32, name="result_second", offset=WORDS_AT + PARTS[2][0] * 4)
         by_unit = [t[:].rearrange("p i (u j) -> p i u j", u=UNITS) for t in (result_first, result_second)]

@@ -55,19 +55,8 @@ def tile_attend_tok_ucb_srt_kernel(tc, qT, k_words, k_scales, bo, offs, out):
         bonus_pool = shared.tile([P, POOL], F32, name="bonus_pool", offset=BONUS_AT)
         scale_pool = shared.tile([P, POOL], U8, name="scale_pool", offset=SCALES_AT)
 
-        ident_narrow = sb.tile([P, P], BF16, name="ident_narrow")
-        nc.vector.memset(ident_narrow[:], 0.0)
         nc.vector.memset(scale_pool[0:SCALE_ROW0, :].bitcast(I32), 0)
         nc.vector.memset(bonus_pool[0:LIVE, :], 0.0)
-        nc.gpsimd.affine_select(
-            out=ident_narrow[:],
-            in_=ident_narrow[:],
-            compare_op=mybir.AluOpType.not_equal,
-            fill=1.0,
-            base=0,
-            pattern=[[-1, P]],
-            channel_multiplier=1,
-        )
         word_pool = shared.tile([P, POOL], U32, name="word_pool", offset=WORDS_AT)
         q_tiles = [shared.tile([P, PACK * EARLY], F32, name="q_early", offset=FIRST_AT)] + [
             shared.tile([P, PACK * UNIT], F32, name="q_late%d" % at, offset=at) for at in (MID_AT, LAST_AT)
@@ -149,6 +138,17 @@ def tile_attend_tok_ucb_srt_kernel(tc, qT, k_words, k_scales, bo, offs, out):
         load_q(1)
         load_q(2)
 
+        ident = shared.tile([P, P], F32, name="ident", offset=PLANE_AT + SLOTS)
+        nc.vector.memset(ident[:], 0.0)
+        nc.gpsimd.affine_select(
+            out=ident[:],
+            in_=ident[:],
+            compare_op=mybir.AluOpType.not_equal,
+            fill=1.0,
+            base=0,
+            pattern=[[-1, P]],
+            channel_multiplier=1,
+        )
         nc.vector.tensor_copy(bonus_row[:], bonus_pool[:].indirect(offsets[:]))
 
         def interleave(c):
@@ -158,8 +158,6 @@ def tile_attend_tok_ucb_srt_kernel(tc, qT, k_words, k_scales, bo, offs, out):
             )
 
         interleave(0)
-        ident = shared.tile([P, P], F32, name="ident", offset=IDENT_AT)
-        nc.scalar.copy(ident[:], ident_narrow[:])
         for r in range(TILES):
             nc.tensor.transpose(bonus_col[:, r, :], bonus_row[:, r * P : (r + 1) * P], ident[:])
         interleave(1)

@@ -187,9 +187,11 @@ def tile_attend_tok_ucb_srt_kernel(tc, qT, k_words, k_scales, bo, offs, out):
 
         for i in range(PAIR):
             add_on_scalar(shifted[:, i * UNIT : (i + 1) * UNIT], held[:, i, :], PAIR + i)
-        for c, h, bank_tag in ((1, 1, "bank6"), (1, 0, "bank0"), (2, 0, "bank1"), (2, 1, "bank2")):
-            target = late[:, :, c - 1 : c, :] if h else first[:, :, c + 1 : c + 2, :]
-            reduce(target, multiply(c, h, both, PARTS[c][0], PARTS[c][1], bank_tag)[:])
+        banks = ("bank6", "bank0", "bank1", "bank2", "bank3", "bank4")
+        steps = [(c, h, i) for c, h in ((1, 1), (1, 0), (2, 0), (2, 1)) for i in both]
+        for n, (c, h, i) in enumerate(steps):
+            target = late[:, i : i + 1, c - 1 : c, :] if h else first[:, i : i + 1, c + 1 : c + 2, :]
+            reduce(target, multiply(c, h, (i,), PARTS[c][0], PARTS[c][1], banks[n % len(banks)])[:])
         result_first = sb.tile([P, PAIR, RUNS], F32, name="result_first")
         result_second = shared.tile([P, PAIR, RUNS], F32, name="result_second", offset=WORDS_AT + PARTS[2][0] * 4)
         by_unit = [t[:].rearrange("p i (u j) -> p i u j", u=UNITS) for t in (result_first, result_second)]
@@ -199,10 +201,6 @@ def tile_attend_tok_ucb_srt_kernel(tc, qT, k_words, k_scales, bo, offs, out):
             add_on_scalar(by_unit[0][:, i, :, :], first[:, i, :, :], i)
         nc.sync.dma_start(out_view[:, 0:PAIR, :], result_first[:])
         reduce(by_unit[1][:, :, 0:1, :], shifted[:, 0 : PAIR * UNIT].rearrange("p (i w) -> p i w", i=PAIR))
-        nc.vector.tensor_tensor(
-            by_unit[1][:, :, 2:UNITS, :],
-            late,
-            bonus_col[:, PAIR:TILES, LIVE:P].unsqueeze(3).to_broadcast([P, PAIR, 2, UNIT_RUNS]),
-            mybir.AluOpType.add,
-        )
+        for i in range(PAIR):
+            add_on_scalar(by_unit[1][:, i, 2:UNITS, :], late[:, i, :, :], PAIR + i)
         nc.sync.dma_start(out_view[:, PAIR:TILES, :], result_second[:])

@@ -55,8 +55,19 @@ def tile_attend_tok_ucb_srt_kernel(tc, qT, k_words, k_scales, bo, offs, out):
         bonus_pool = shared.tile([P, POOL], F32, name="bonus_pool", offset=BONUS_AT)
         scale_pool = shared.tile([P, POOL], U8, name="scale_pool", offset=SCALES_AT)
 
+        ident = sb.tile([P, P], F32, name="ident")
+        nc.vector.memset(ident[:], 0.0)
         nc.vector.memset(scale_pool[0:SCALE_ROW0, :].bitcast(I32), 0)
         nc.vector.memset(bonus_pool[0:LIVE, :], 0.0)
+        nc.gpsimd.affine_select(
+            out=ident[:],
+            in_=ident[:],
+            compare_op=mybir.AluOpType.not_equal,
+            fill=1.0,
+            base=0,
+            pattern=[[-1, P]],
+            channel_multiplier=1,
+        )
         word_pool = shared.tile([P, POOL], U32, name="word_pool", offset=WORDS_AT)
         q_tiles = [shared.tile([P, PACK * EARLY], F32, name="q_early", offset=FIRST_AT)] + [
             shared.tile([P, PACK * UNIT], F32, name="q_late%d" % at, offset=at) for at in (MID_AT, LAST_AT)
@@ -78,7 +89,7 @@ def tile_attend_tok_ucb_srt_kernel(tc, qT, k_words, k_scales, bo, offs, out):
         for lo, hi in ((0, PREFIX), (PREFIX, POOL)):
             nc.sync.dma_start(word_pool[:, lo:hi].bitcast(I32), words[:, lo:hi])
 
-        bonus_row = sb.tile([P, SLOTS], F32, name="bonus_row")
+        bonus_row = [sb.tile([P, HALF], F32, name="bonus_row%d" % h) for h in range(2)]
         picked = sb.tile([P, SLOTS], U8, name="picked")
         grouped_early = sb.tile([P, EARLY * PACK], BF16, name="grouped_early", align_bytes=64)
         k_codes = [
@@ -138,18 +149,9 @@ def tile_attend_tok_ucb_srt_kernel(tc, qT, k_words, k_scales, bo, offs, out):
         load_q(1)
         load_q(2)
 
-        ident = shared.tile([P, P], F32, name="ident", offset=PLANE_AT + SLOTS)
-        nc.vector.memset(ident[:], 0.0)
-        nc.gpsimd.affine_select(
-            out=ident[:],
-            in_=ident[:],
-            compare_op=mybir.AluOpType.not_equal,
-            fill=1.0,
-            base=0,
-            pattern=[[-1, P]],
-            channel_multiplier=1,
-        )
-        nc.vector.tensor_copy(bonus_row[:], bonus_pool[:].indirect(offsets[:]))
+        for h in range(2):
+            entries = offsets[:, h * HALF // LIST_ROWS : (h + 1) * HALF // LIST_ROWS]
+            nc.vector.tensor_copy(bonus_row[h][:], bonus_pool[:].indirect(entries))
 
         def interleave(c):
             nc.scalar.copy(
@@ -159,7 +161,7 @@ def tile_attend_tok_ucb_srt_kernel(tc, qT, k_words, k_scales, bo, offs, out):
 
         interleave(0)
         for r in range(TILES):
-            nc.tensor.transpose(bonus_col[:, r, :], bonus_row[:, r * P : (r + 1) * P], ident[:])
+            nc.tensor.transpose(bonus_col[:, r, :], bonus_row[r // PAIR][:, (r % PAIR) * P : (r % PAIR + 1) * P], ident[:])
         interleave(1)
         interleave(2)
 

@@ -83,9 +83,9 @@ def tile_attend_tok_ucb_srt_kernel(tc, qT, k_words, k_scales, bo, offs, out):
             nc.sync.dma_start(q_raw[c], q_rows[:, :, lo:hi])
 
         nc.sync.dma_start(offsets[:], offs)
-        nc.sync.dma_start(scale_pool[SCALE_ROW0:P, :].bitcast(I32), scales)
-        nc.scalar.dma_start(bonus_pool[LIVE:P, :], bo[LIVE:P, :])
+        nc.scalar.dma_start(scale_pool[SCALE_ROW0:P, :].bitcast(I32), scales)
         load_q(0)
+        nc.sync.dma_start(bonus_pool[LIVE:P, :], bo[LIVE:P, :])
         for lo, hi in ((0, PREFIX), (PREFIX, POOL)):
             nc.sync.dma_start(word_pool[:, lo:hi].bitcast(I32), words[:, lo:hi])
 

from contextlib import ExitStack

import concourse.mybir as mybir

F32 = mybir.dt.float32
BF16 = mybir.dt.bfloat16
I32 = mybir.dt.int32
U32 = mybir.dt.uint32
U16 = mybir.dt.uint16
U8 = mybir.dt.uint8
FP8X4 = mybir.dt.float8_e4m3fn_x4

P = 128
PACK = 4
SLOTS, POOL, D, NQ, SEG = 512, 2048, 512, 512, 16
RUNS = NQ // SEG
TILES = SLOTS // P
PAIR = 2
HALF = PAIR * P
LIST_ROWS = 16
QUADRANTS, QUADRANT, SCALE_ROWS = 4, 32, 4
PREFIX = POOL - HALF
LIVE = P - 1
SCALE_ROW0 = P - D // 32
UNIT = 128
UNITS = NQ // UNIT
UNIT_RUNS = UNIT // SEG
PARTS = ((0, 2 * UNIT), (2 * UNIT, 3 * UNIT), (3 * UNIT, NQ))
EARLY = PARTS[0][1]

LAP = 64
RAW_BYTES = PACK * UNIT * 4
MID_AT = 0
SCALES_AT = RAW_BYTES - LAP
PLANE_AT = RAW_BYTES
LAST_AT = SCALES_AT + POOL - LAP
WORDS_AT = LAST_AT + RAW_BYTES
BONUS_AT = WORDS_AT + POOL * 4
FIRST_AT = BONUS_AT + POOL * 4
IDENT_AT = FIRST_AT - P * 2
CODES_AT = FIRST_AT + P * 2

FLOPS = 2 * SLOTS * D * NQ
BYTES = D * NQ * 4 + P * POOL * 4 + (D // 32) * POOL + POOL * 4 + P * (SLOTS // LIST_ROWS) * 2 + SLOTS * RUNS * 4


def tile_attend_tok_ucb_srt_kernel(tc, qT, k_words, k_scales, bo, offs, out):
    nc = tc.nc
    with ExitStack() as ctx:
        sb = ctx.enter_context(tc.tile_pool(name="sb", bufs=1))
        shared = ctx.enter_context(tc.tile_pool(name="shared", bufs=1))
        ps = ctx.enter_context(tc.psum_pool(name="ps", bufs=1))

        offsets = sb.tile([P, SLOTS // LIST_ROWS], U16, name="offsets")
        bonus_pool = shared.tile([P, POOL], F32, name="bonus_pool", offset=BONUS_AT)
        scale_pool = shared.tile([P, POOL], U8, name="scale_pool", offset=SCALES_AT)

        ident = sb.tile([P, P], F32, name="ident")
        nc.vector.memset(ident[:], 0.0)
        nc.vector.memset(scale_pool[0:SCALE_ROW0, :].bitcast(I32), 0)
        nc.vector.memset(bonus_pool[0:LIVE, :], 0.0)
        nc.gpsimd.affine_select(
            out=ident[:],
            in_=ident[:],
            compare_op=mybir.AluOpType.not_equal,
            fill=1.0,
            base=0,
            pattern=[[-1, P]],
            channel_multiplier=1,
        )
        word_pool = shared.tile([P, POOL], U32, name="word_pool", offset=WORDS_AT)
        q_tiles = [shared.tile([P, PACK * EARLY], F32, name="q_early", offset=FIRST_AT)] + [
            shared.tile([P, PACK * UNIT], F32, name="q_late%d" % at, offset=at) for at in (MID_AT, LAST_AT)
        ]
        q_raw = [t[:].rearrange("p (t w) -> p t w", t=PACK) for t in q_tiles]

        q_rows = qT[0].rearrange("(p t) w -> p t w", t=PACK)
        words = k_words[0].rearrange("p n t -> p (n t)").bitcast(I32)
        scales = k_scales[0].bitcast(I32)

        def load_q(c):
            lo, hi = PARTS[c]
            nc.sync.dma_start(q_raw[c], q_rows[:, :, lo:hi])

        nc.sync.dma_start(offsets[:], offs)
        nc.scalar.dma_start(scale_pool[SCALE_ROW0:P, :].bitcast(I32), scales)
        load_q(0)
        nc.sync.dma_start(bonus_pool[LIVE:P, :], bo[LIVE:P, :])
        for lo, hi in ((0, PREFIX), (PREFIX, POOL)):
            nc.sync.dma_start(word_pool[:, lo:hi].bitcast(I32), words[:, lo:hi])

        bonus_row = [sb.tile([P, HALF], F32, name="bonus_row%d" % h) for h in range(2)]
        picked = sb.tile([P, SLOTS], U8, name="picked")
        grouped_early = sb.tile([P, EARLY * PACK], BF16, name="grouped_early", align_bytes=64)
        k_codes = [
            shared.tile([P, HALF], U32, name="k_codes%d" % h, align_bytes=64, offset=CODES_AT + h * HALF * 4)
            for h in range(2)
        ]
        bonus_col = ps.tile([P, TILES, P], F32, name="bonus_col")
        grouped_late = sb.tile([P, (NQ - EARLY) * PACK], BF16, name="grouped_late", align_bytes=64)
        grouped = [grouped_early[:]] + [
            grouped_late[:, (lo - EARLY) * PACK : (hi - EARLY) * PACK] for lo, hi in PARTS[1:]
        ]
        q_codes = [sb.tile([P, EARLY], U32, name="q_codes0", align_bytes=64)] + [
            shared.tile([P, hi - lo], U32, name="q_codes%d" % lo, align_bytes=64, offset=WORDS_AT + lo * 4)
            for lo, hi in PARTS[1:]
        ]
        q_scale = [sb.tile([P, hi - lo], U8, name="q_scale%d" % lo, align_bytes=64) for lo, hi in PARTS]
        cells = PAIR * UNIT_RUNS
        best_first = sb.tile([P, UNITS * cells], F32, name="best_first")
        best_mid = shared.tile([P, cells], F32, name="best_mid", offset=MID_AT)
        best_late = shared.tile([P, 2 * cells], F32, name="best_late", offset=LAST_AT + RAW_BYTES - 2 * cells * 4)
        first, mid, late = (
            t[:].rearrange("p (u i j) -> p i u j", i=PAIR, j=UNIT_RUNS) for t in (best_first, best_mid, best_late)
        )
        out_view = out[0].rearrange("(r p) j -> p r j", p=P)

        def multiply(c, h, tiles, lo, hi, bank_tag):
            bank = ps.tile([P, len(tiles), hi - lo], F32, name="scores", tag=bank_tag)
            rows = slice(lo - PARTS[c][0], hi - PARTS[c][0])
            for n, i in enumerate(tiles):
                r = PAIR * h + i
                nc.tensor.matmul_mx(
                    out=bank[:, n, :],
                    lhsT=k_codes[h][:, i * P : (i + 1) * P].bitcast(FP8X4),
                    lhsT_scale=k_scale[:, r * P : (r + 1) * P],
                    rhs=q_codes[c][:, rows].bitcast(FP8X4),
                    rhs_scale=q_scale[c][:, rows],
                    start=True,
                    stop=True,
                )
            return bank

        def reduce(target, scores):
            nc.vector.tensor_reduce(
                target,
                scores.rearrange("p i (u j s) -> p i u j s", j=UNIT_RUNS, s=SEG),
                axis=mybir.AxisListType.X,
                op=mybir.AluOpType.max,
            )

        nc.vector.tensor_copy(picked[:], scale_pool[:].indirect(offsets[:]))
        k_scale = shared.tile([P, SLOTS], U8, name="k_scale", align_bytes=64, offset=PLANE_AT)
        for quad in range(QUADRANTS):
            src, dst = SCALE_ROW0 + SCALE_ROWS * quad, QUADRANT * quad
            nc.sync.dma_start(
                k_scale[dst : dst + SCALE_ROWS, :].bitcast(I32), picked[src : src + SCALE_ROWS, :].bitcast(I32)
            )
        load_q(1)
        load_q(2)

        for h in range(2):
            entries = offsets[:, h * HALF // LIST_ROWS : (h + 1) * HALF // LIST_ROWS]
            nc.vector.tensor_copy(bonus_row[h][:], bonus_pool[:].indirect(entries))

        def interleave(c):
            nc.scalar.copy(
                grouped[c].rearrange("p (w i t) -> p w t i", i=4, t=PACK),
                q_raw[c].rearrange("p t (w i) -> p w t i", i=4),
            )

        interleave(0)
        for r in range(TILES):
            nc.tensor.transpose(bonus_col[:, r, :], bonus_row[r // PAIR][:, (r % PAIR) * P : (r % PAIR + 1) * P], ident[:])
        interleave(1)
        interleave(2)

        def quantise(c):
            nc.vector.quantize_mx(out=q_codes[c][:].bitcast(FP8X4), scales=q_scale[c][:], in_=grouped[c])

        quantise(0)
        nc.vector.tensor_copy(k_codes[0][:], word_pool[:, 0:PREFIX].indirect(offsets[:, 0 : HALF // LIST_ROWS]))
        nc.vector.tensor_copy(k_codes[1][:], word_pool[:].indirect(offsets[:, HALF // LIST_ROWS :]))
        both = (0, 1)
        for i in range(PAIR):
            for u in range(EARLY // UNIT):
                scores = multiply(0, 0, (i,), u * UNIT, (u + 1) * UNIT, "bank%d" % (2 * i + u))
                reduce(first[:, i : i + 1, u : u + 1, :], scores[:])
        quantise(1)
        reduce(mid, multiply(0, 1, both, UNIT, EARLY, "bank4")[:])
        held = multiply(0, 1, both, 0, UNIT, "bank5")
        quantise(2)
        shifted = shared.tile([P, PAIR * UNIT + TILES], F32, name="shifted", offset=LAST_AT)
        bonus = shifted[:, PAIR * UNIT :]
        nc.scalar.copy(bonus, bonus_col[:, :, LIVE])

        def add_on_scalar(target, source, r):
            nc.scalar.activation(target, source, mybir.ActivationFunctionType.Identity, bias=bonus[:, r : r + 1])

        for i in range(PAIR):
            add_on_scalar(shifted[:, i * UNIT : (i + 1) * UNIT], held[:, i, :], PAIR + i)
        banks = ("bank6", "bank0", "bank1", "bank2", "bank3", "bank4")
        steps = [(c, h, i) for c, h in ((1, 1), (1, 0), (2, 0), (2, 1)) for i in both]
        for n, (c, h, i) in enumerate(steps):
            target = late[:, i : i + 1, c - 1 : c, :] if h else first[:, i : i + 1, c + 1 : c + 2, :]
            reduce(target, multiply(c, h, (i,), PARTS[c][0], PARTS[c][1], banks[n % len(banks)])[:])
        result_first = sb.tile([P, PAIR, RUNS], F32, name="result_first")
        result_second = shared.tile([P, PAIR, RUNS], F32, name="result_second", offset=WORDS_AT + PARTS[2][0] * 4)
        by_unit = [t[:].rearrange("p i (u j) -> p i u j", u=UNITS) for t in (result_first, result_second)]
        for i in range(PAIR):
            add_on_scalar(by_unit[1][:, i, 1, :], mid[:, i, 0, :], PAIR + i)
        for i in range(PAIR):
            add_on_scalar(by_unit[0][:, i, :, :], first[:, i, :, :], i)
        nc.sync.dma_start(out_view[:, 0:PAIR, :], result_first[:])
        reduce(by_unit[1][:, :, 0:1, :], shifted[:, 0 : PAIR * UNIT].rearrange("p (i w) -> p i w", i=PAIR))
        for i in range(PAIR):
            add_on_scalar(by_unit[1][:, i, 2:UNITS, :], late[:, i, :, :], PAIR + i)
        nc.sync.dma_start(out_view[:, PAIR:TILES, :], result_second[:])
